import numpy as np, ml_dtypes
CORES = [25,29,65,69,153,157,193,197]
N = 8
import mx_ref
BF = ml_dtypes.bfloat16
def gcols(t, e):
    v = np.concatenate([t.reshape(8, 16, -1, 4), np.zeros((8, 16, 1, 4), BF)], axis=2)
    return np.ascontiguousarray(np.stack([v[g][:, e[g]] for g in range(8)])).reshape(128, -1)
def tile(rs):
    return np.stack(rs, axis=2).reshape(128, -1).astype(BF)
def pick(q, e):
    c = np.concatenate([q[0].reshape(128, -1, 4), np.zeros((128, 1, 4), np.uint8)], axis=1); s = np.concatenate([q[1], np.ones((16, 1), np.uint8)], axis=1)
    return (np.ascontiguousarray(c[:, e].reshape(128, -1)), np.ascontiguousarray(s[:, e]))
def join(*qs):
    return (np.concatenate([q[0] for q in qs], axis=1), np.concatenate([q[1] for q in qs], axis=1))
def put(q, e, v):
    c, s = q[0].reshape(128, -1, 4).copy(), q[1].copy(); c[:, e] = v[0].reshape(128, -1, 4); s[:, e] = v[1]
    return (c.reshape(128, -1), s)
def pk(c, s):
    return (np.ascontiguousarray(c), mx_ref.live(s))
def emit(q):
    return q[0], q[1]
def packed(v, rng):
    q = [mx_ref.quantize(np.ascontiguousarray(v[r])) for r in range(N)]
    return np.stack([a for a, b in q]), np.stack([mx_ref.plane(b, rng) for a, b in q])
def values_of_codes():
    e, c = np.zeros((128, 128, 4), np.float32), np.zeros((128, 2, 4), np.uint8)
    e[np.arange(128), np.arange(128), 0] = 1
    c[:127, :, 0] = np.arange(256).reshape(2, 128).T[:127]
    return mx_ref.matmul(mx_ref.quantize(e.reshape(128, 512).astype(BF)), (c.reshape(128, 8), np.full((16, 2), 127, np.uint8))).T.reshape(-1).astype(np.float64)
CODE_VALUE, SCALE_VALUE = values_of_codes(), 2.0 ** (np.arange(256) - 127.0)
def decode(q):
    return (CODE_VALUE[q[0]].reshape(16, 8, -1, 4) * SCALE_VALUE[q[1]][:, None, :, None] + 0.0).reshape(128, -1).astype(np.float32)
def f(rng, *shape):
    return mx_ref.flush((rng.standard_normal(shape, dtype=np.float32) * np.exp2(rng.integers(-2, 3, shape[:-1] + (1,)))).astype(BF))
def wide(rng, *shape, cols=0):
    v = rng.standard_normal(shape, dtype=np.float32) * np.exp2(rng.integers(-12, 13, shape)).astype(np.float32)
    if cols: v *= np.repeat(np.exp2(rng.integers(-cols, cols + 1, shape[:-2] + (1, shape[-1] // 4))) * (rng.random(shape[:-2] + (1, shape[-1] // 4)) > 0.0625), 4, axis=-1).astype(np.float32)
    return mx_ref.flush(v.astype(BF))
C, K, DEP, R = 288, 128, 36, 3
SOURCE = [7, 0, 1, 1, 2, 2, 3, 3]
LEVEL = [0, 1, 2, 2, 3, 3, 3, 3]
ITEM = 8 * (np.arange(C) % DEP) + np.arange(C) // DEP
def big(v):
    v = v.astype(np.float32)
    v[np.abs(v) < np.float32(2.0 ** -16)] = 0
    return v.astype(BF)
def numbers_of(rng):
    return {"x": big(f(rng, N, 128, 4 * C)), "u": np.array(f(rng, N, 128, 512)), "v": np.array(f(rng, N, 128, 512))}
def layers(rng):
    return big(f(rng, N, 128, 2048).astype(np.float32) * np.float32(0.5)).reshape(N, 8, 16, 4, 8, 16, 4)
def weights(rng, w):
    c, p = packed(np.ascontiguousarray(w).reshape(N, 128, 2048), rng)
    return {"wc": c, "ws": p}
def own_bits(u):
    for b in range(3): u[:, :, b::16] = 0
    for h in range(0, 128, 16):
        for b in range(3): u[:, h, h + b, b] = 1
def setup_inputs(rng):
    return {**numbers_of(rng), **weights(rng, layers(rng))}
def setup_inputs_ties(rng):
    d = numbers_of(rng)
    e = rng.permutation(N)
    k = rng.integers(-1, 2, (N, 8, C, 3)).astype(np.float32)
    k[e[0]] = 0
    k[e[1]] = 1
    for g in range(8): k[e[2], g, :, 0] = 2.0 * (LEVEL[g] % 2) - 1.0
    x = d["x"].reshape(N, 8, 16, C, 4)
    x[:, :, :8] = 0
    x[:, :, 0, :, :3] = k.astype(BF)
    u = d["u"].reshape(N, 128, 128, 4)
    own_bits(u)
    w = layers(rng)
    w[:, :, :, :, :, :8] = 0
    return {"x": x.reshape(N, 128, 4 * C), "u": u.reshape(N, 128, 512), "v": d["v"], **weights(rng, w)}
def setup_inputs_near(rng):
    d = numbers_of(rng)
    x = d["x"].reshape(N, 8, 16, C, 4)
    u = d["u"].reshape(N, 128, 128, 4)
    o = rng.permutation(N) % 4
    x[:, :, :8] = 0
    for b in range(3): u[:, :, b::16] = 0
    for r in range(N):
        a = rng.integers(-1, 2, (8, C, 3)).astype(np.float32)
        b = np.where(rng.random((8, C, 3)) < 0.75, -a, rng.integers(-1, 2, (8, C, 3))).astype(np.float32)
        k = np.float32(2.0 ** -27 if o[r] < 2 else 1.0)
        a, b = a * k, b * k
        for g in rng.permutation(8)[:4]: a[g, rng.integers(C)] = 2.0 ** 18 * rng.choice([-1.0, 1.0], 3)
        x[r, :, 0, :, :3] = a.astype(BF)
        x[r, :, 1, :, :3] = b.astype(BF)
        m = 2.0 ** -30 if o[r] % 2 == 0 else 1.0
        for h in range(0, 128, 16):
            for t in range(3):
                u[r, h, h + t, t] = 1.125 * m
                u[r, h + 1, h + t, t] = m
    w = layers(rng)
    w[:, :, :8] = 0
    w[:, :, :, :, :, :8] = 0
    return {"x": x.reshape(N, 128, 4 * C), "u": u.reshape(N, 128, 512), "v": d["v"], **weights(rng, w)}
def setup_inputs_late(rng):
    d = numbers_of(rng)
    s = rng.integers(6, 8, (N, 8, 8, DEP))
    for g in range(8):
        if g: s[:, g, :, 0] = LEVEL[g] - 1
        s[:, g, :, -1] = LEVEL[g]
    s[:, 7, 7] = 0
    s[:, 7, 7, -1] = 2
    e = int(rng.integers(N))
    s[e] = 7
    for g in range(8):
        if LEVEL[g] > 0: s[e, g, :, 0] = 7 - LEVEL[g]
        if LEVEL[g] < 3: s[e, g, :, -1] = 6 - LEVEL[g]
    s[e, 2:4, :7, -1] = 2
    for h in (0, 1, 6, 7):
        s[e, 4:, h, 0] = 2
        s[e, 4:, h, 1] = 3
    s[e, 4:, 5, 1] = 6
    s = s.reshape(N, 8, C)
    x = d["x"].reshape(N, 8, 16, C, 4)
    x[:, :, :8] = 0
    x[:, :, 0, :, :3] = (2.0 * ((s[..., None] >> np.array([2, 1, 0])) & 1) - 1.0).astype(np.float32).astype(BF)
    k = (1.0 + (2 * rng.integers(0, 64, (N, 8, 8, C, 4)) + 1) / 128.0) * np.exp2(-1.0 * rng.integers(8, 15, (N, 8, 8, C, 4))) * rng.choice([-1.0, 1.0], (N, 8, 8, C, 4))
    k[:, :, 0, :, 0] = 1.96875
    x[:, :, 8:] = k.astype(np.float32).astype(BF)
    u = d["u"].reshape(N, 128, 128, 4)
    own_bits(u)
    w = layers(rng)
    w[:, :, :, :, :, :8] = 0
    return {"x": x.reshape(N, 128, 4 * C), "u": u.reshape(N, 128, 512), "v": d["v"], **weights(rng, w)}
def setup_inputs_ends(rng):
    o = rng.permutation(N)
    x = rng.choice([-1.0, 1.0], (N, 8, 1, C, 1)) * np.ones((1, 1, 16, 1, 4))
    u, v = rng.choice([-1.0, 1.0], (N, 128, 512)), rng.choice([-1.0, 1.0], (N, 128, 512))
    w = np.zeros((N, 128, 2048), np.float32)
    for r in range(N):
        if o[r] == 0: x[r] = 1.0
        if o[r] == 3: x[r] = -1.0
        if o[r] in (0, 3): u[r] = 1.0
        x[r] *= 2.0 ** 19 if o[r] % 2 == 0 else 2.0 ** -27
        u[r] *= 2.0 ** 30 if o[r] % 4 < 2 else 2.0 ** -30
        v[r] *= 2.0 ** 30 if o[r] % 4 in (0, 3) else 2.0 ** -30
        w[r] = (2.0, -2.0, 0.0)[o[r] % 3]
    return {"x": x.astype(np.float32).reshape(N, 128, 4 * C).astype(BF), "u": u.astype(np.float32).astype(BF), "v": v.astype(np.float32).astype(BF), **weights(rng, w.astype(BF))}
def setup_inputs_spread(rng):
    d = setup_inputs(rng)
    d["x"] = big(wide(rng, N, 128, 4 * C, cols=3))
    return d
def check_inputs(d):
    b = []
    for k, m in (("x", 2.0 ** 19), ("u", 2.0 ** 30), ("v", 2.0 ** 30)):
        a = np.abs(d[k].astype(np.float32))
        if not (np.isfinite(a).all() and ((a == 0) | (a >= 2.0 ** -30) & (a <= m)).all()): b.append("a value of " + k)
    none, least, most = [emit(mx_ref.quantize(np.full((128, 16), k, np.float32).astype(BF)))[1][0, 0] for k in (0.0, 2.0 ** -30, 2.0 ** 30)]
    for r in range(N):
        if ((d["wc"][r] == 0x7F) | (d["wc"][r] == 0xFF)).any(): b.append("wc: a code that is no number")
        s = mx_ref.live(d["ws"][r])
        if ((s != none) & ((s < least) | (s > most))).any(): b.append("ws: a scale out of range")
        a = np.abs(decode(pk(d["wc"][r], d["ws"][r])).astype(np.float64)).reshape(128, 512, 4)
        if not (np.sum(a, axis=(0, 2)) <= 1024).all(): b.append("W: a column that adds up to more than 1024")
    return b
def times(sym, wait):
    sym, wait = sym.reshape(8, DEP), wait.reshape(8, DEP)
    t, last = np.zeros((8, DEP), np.int64), np.zeros(8, np.int64)
    for i in range(DEP):
        last = np.maximum(last, wait[:, i]) + (1 + sym[:, i])
        t[:, i] = last
    return t.reshape(C)
def orders(sym):
    o, b = np.zeros((8, C), np.int64), np.zeros((8, K), np.int64)
    first, least = np.full((8, 8), -1), np.zeros((8, 8), np.int64)
    for g in range(8):
        e = SOURCE[g]
        t = times(sym[g], least[e][sym[g]] if g > 0 else np.zeros(C, np.int64))
        o[g] = np.argsort(t, kind="stable")
        for s in range(8):
            p = np.flatnonzero(sym[g][o[g]] == s)
            if len(p) > 0:
                first[g, s] = o[g, p[0]]
                least[g, s] = t[o[g, p[0]]]
        l = o[g, :K]
        p = first[e][sym[g][l]] if g > 0 else l
        b[g] = np.where(p < 0, l, p)
    return o, b
def reference(x, u, v, wc, ws):
    qu = [mx_ref.quantize(u[r]) for r in range(N)]
    lay = [pk(wc[r], ws[r]) for r in range(N)]
    now = [x[r] for r in range(N)]
    order = np.zeros((N, 8, C), np.int64)
    for t in range(R):
        stay, sent = [], []
        for r in range(N):
            q = mx_ref.quantize(now[r])
            full = decode(q)
            s = mx_ref.matmul(qu[r], q)
            order[r], mate = orders(4 * (s[::16] > 0) + 2 * (s[1::16] > 0) + (s[2::16] > 0))
            a = full.reshape(8, 16, C, 4)
            z = np.stack([(a[g][:, order[r, g, :K]] + a[SOURCE[g]][:, mate[g]]) * np.float32(0.5) for g in range(8)])
            sent.append(mx_ref.quantize(np.ascontiguousarray(z.reshape(128, 4 * K).astype(BF))))
            stay.append(gcols(full.astype(BF), order[r][:, K:]))
        for r in range(N):
            q = sent[r - 1]
            d = decode(q)
            h = tile([mx_ref.matmul(pick(lay[r], np.arange(128 * b, 128 * b + 128)), q) * np.float32(0.0078125) + d[:, b::4] for b in range(4)])
            items = np.concatenate([stay[r], h], axis=1).reshape(128, C, 4)
            now[r] = np.ascontiguousarray(items[:, ITEM].reshape(128, 4 * C))
    y, op = np.zeros((N, 128, C), np.float32), np.zeros((N, 8, C), np.float32)
    oc, osc = np.zeros((N, 128, 4 * C), np.uint8), np.zeros((N, 16, C), np.uint8)
    for r in range(N):
        q = mx_ref.quantize(now[r])
        y[r] = mx_ref.matmul(mx_ref.quantize(v[r]), q)
        op[r] = order[r]
        oc[r], osc[r] = emit(q)
    return {"y": y, "op": op, "oc": oc, "osc": osc}

@@ -1,0 +1,555 @@
+from concourse.bass import DstId, RemoteDMATransfer
+from concourse.mybir import dt, AluOpType, AxisListType, ActivationFunctionType
+
+OP = AluOpType
+CP = ActivationFunctionType.Copy
+C, K, R, NS, NH = 288, 128, 3, 160, 128
+NA = 13
+NV = 18 - NA
+THR = 1572864.0
+BIG = 2097152.0
+
+
+def magic(step):
+    return float(1.5 * 2.0 ** 23 * step)
+
+
+SCRATCH = {}
+
+
+def buf(name, n, dtype="float32", where="sbuf"):
+    SCRATCH[name] = (where, [128, n], dtype)
+
+
+CODE = "float8_e4m3fn_x4"
+
+
+def pair(name, n):
+    buf("q" + name, n, CODE)
+    buf("s" + name, n, "uint8")
+
+
+for _b in range(8):
+    buf("ps%d" % _b, 512, "float32", "psum")
+buf("xt", 4 * C, "bfloat16"); buf("ut", 512, "bfloat16"); buf("vt", 512, "bfloat16")
+pair("u0", 128); pair("u", 128); pair("v", 128); pair("w", 512); pair("x", C); pair("n", C); pair("f", 306)
+CONST = {n: 128 * i for i, n in enumerate(["m0", "m1", "m2", "m3", "p0", "p1", "p2", "k1", "k2", "k3",
+                                           "e0", "e1", "e2", "e3", "h0", "h1", "h2", "h3"])}
+pair("k", 128 * len(CONST))
+for _l in (1, 2, 3):
+    buf("kt%d" % _l, 512, "bfloat16")
+    buf("list%d" % _l, 18, "uint16")
+    buf("thr%d" % _l, 32)
+pair("z", R * K); pair("a", R * K)
+buf("rq", 32 * R, CODE); buf("rs", K * R, "uint8")
+buf("pc", 64); buf("st", 512, "bfloat16"); buf("zero", 680, "bfloat16")
+buf("gm0", 128); buf("gm1", 128); buf("gm2", 128); buf("gm3", 128)
+buf("m8", 128, "int32"); buf("mb", 128, "int32"); buf("mc", 128, "int32"); buf("xp", 128); buf("eq", 128)
+buf("i3", 128)
+for _t in range(4):
+    buf("ct%d" % _t, 128)
+buf("one", 128, "bfloat16"); buf("idt", 520, "bfloat16"); buf("ids", 520, "bfloat16")
+buf("onef", C); buf("j16", C); buf("j4", C); buf("mask16", C); buf("mask4", C); buf("r16", C); buf("r4", C)
+buf("r144", C, "bfloat16")
+buf("d0a", C); buf("d0b", C); buf("own", C); buf("z32", 32)
+buf("jn", 18); buf("jk", 18); buf("nat", 18, "uint16")
+buf("ja", 8); buf("jb", 8); buf("ul", 8, "uint16")
+buf("fls", 680, "bfloat16"); buf("flh", 544, "bfloat16")
+buf("t", C); buf("wt", C); buf("pv", C); buf("sm", 16); buf("bc", 32); buf("tr", 32); buf("bcb", 32); buf("trb", 32)
+buf("val", C); buf("ex", C); buf("scx", C); buf("cf", NV * C, "bfloat16"); buf("cs", NV * C, "bfloat16")
+buf("junk", NA * C, "bfloat16"); buf("acc", NA); buf("rkv", NV); buf("off", 18, "uint16")
+buf("lin", C); buf("ml", C); buf("sc", C)
+buf("ta", 40); buf("oa", 40); buf("la", 32); buf("lb", 32); buf("lu", 32, "uint16"); buf("bu", 32, "uint16")
+buf("tsv", 40); buf("osv", 40); buf("sul", 40, "uint16")
+buf("fh", 4 * C, "bfloat16"); buf("fp", 8 * C, "bfloat16")
+buf("g1", 512); buf("zt", 512, "bfloat16"); buf("xs", 640, "bfloat16"); buf("xh", 512, "bfloat16")
+buf("tm", 512); buf("o1", C); buf("o2", C); buf("o3", C); buf("o4", C); buf("opt", C); buf("yt", C)
+
+SEMAPHORES = ["ev", "ea", "ep", "eg", "lx", "lu", "lw", "lws", "lv", "fpd", "od", "snt"]
+SEMAPHORES += ["arr%d" % _r for _r in range(R)] + ["rar%d" % _r for _r in range(R)]
+
+
+def relays(topo, a, b):
+    if topo.may_write(a, b):
+        return []
+    return [c for c in topo.cores_of(a) if c != a and topo.may_write(c, b)]
+
+
+def bits(es):
+    return sum(1 << e for e in es)
+
+
+def u8(ap):
+    return ap.bitcast(dt.uint8)
+
+
+def relay_program(g, core, T, topo):
+    for i, a in enumerate(T.cores):
+        b = T.cores[(i + 1) % len(T.cores)]
+        rl = relays(topo, a, b)
+        if core not in rl:
+            continue
+        j = rl.index(core)
+        hop = topo.engines(a, core)
+        rid, pid = topo.addr(b, core)
+        es = topo.engines(core, b)
+        total = 0
+        for r in range(R):
+            g.wait_ge(T.sem["rar%d" % r], 2 + (len(hop) // 2 if j == 0 else 0))
+            tr = [RemoteDMATransfer(dst_ids=[DstId(rid=rid, pnc=pid)], dma_engine_mask=bits(es[::2]), remote_sem=T.sem["arr%d" % r],
+                                    src=u8(T.rq[:, 32 * r:32 * r + 32]), dst=u8(T.qa[:, K * r + 32 * j:K * r + 32 * j + 32]))]
+            if j == 0:
+                tr.append(RemoteDMATransfer(dst_ids=[DstId(rid=rid, pnc=pid)], dma_engine_mask=bits(es[1::2]), remote_sem=T.sem["arr%d" % r],
+                                            src=T.rs[:, K * r:K * r + K], dst=T.sa[:, K * r:K * r + K]))
+            g.remote_dma_fused(tr, local_sem=T.sem.snt)
+            total += len(es) // 2 * len(tr)
+        g.wait_ge(T.sem.snt, total)
+
+
+def rank_program(g, core, T, topo):
+    rank = T.rank_of(core)
+    if rank is None:
+        relay_program(g, core, T, topo)
+        return
+    N = len(T.cores)
+    nxt, prv = T.cores[(rank + 1) % N], T.cores[(rank - 1) % N]
+    queue = {"v": g.vector, "a": g.scalar, "p": g.tensor, "g": g, "sy": g.sync}
+    count = {}
+    known = {q: {} for q in queue}
+    wr, rd = {}, {}
+
+    def emit(q, fn, reads, writes, sem=None, inc=1):
+        sem = sem or "e" + q
+        need = {}
+
+        def dep(d):
+            need[d[1]] = max(need.get(d[1], 0), d[2])
+        for k in reads:
+            for d in wr.get(k, []):
+                dep(d)
+            if k.startswith("ps"):
+                for d in rd.get(k, []):
+                    if d[0] != q:
+                        dep(d)
+        for k in writes:
+            for d in wr.get(k, []) + rd.get(k, []):
+                dep(d)
+        for s in need:
+            if known[q].get(s, 0) < need[s]:
+                queue[q].wait_ge(T.sem[s], need[s])
+                known[q][s] = need[s]
+        ins = fn()
+        if ins is None:
+            return
+        ins.then_inc(T.sem[sem], inc)
+        count[sem] = count.get(sem, 0) + inc
+        d = (q, sem, count[sem])
+        for k in writes:
+            wr[k] = [d]
+            rd[k] = []
+        for k in reads:
+            rd[k] = [e for e in rd.get(k, []) if e[1] != sem] + [d]
+
+    v, s_, te = g.vector, g.scalar, g.tensor
+
+    def ts(out, in0, s1, s2, op0, op1, reads, writes):
+        if op1 is None:
+            emit("v", lambda: v.tensor_scalar(out, in0, s1, None, op0), reads, writes)
+        else:
+            emit("v", lambda: v.tensor_scalar(out, in0, s1, s2, op0, op1), reads, writes)
+
+    def tt(out, in0, in1, op, reads, writes):
+        emit("v", lambda: v.tensor_tensor(out, in0, in1, op), reads, writes)
+
+    def scan(out, d0, d1, init, op0, op1, reads, writes):
+        emit("v", lambda: v.tensor_tensor_scan(out, d0, d1, init, op0, op1), reads, writes)
+
+    def quant(name, a, b, tile, reads, writes):
+        if name in CONST:
+            a, b, name = CONST[name] + a, CONST[name] + b, "k"
+        emit("v", lambda: v.quantize_mx(T["q" + name][:, a:b], T["s" + name][:, a:b], tile), reads, writes)
+
+    def act(out, in_, reads, writes, scale=1.0):
+        emit("a", lambda: s_.activation(out, in_, CP, scale=scale), reads, writes)
+
+    def mm(bank, n, st, so, mv, a, reads):
+        if st in CONST:
+            so, st = CONST[st], "k"
+        emit("p", lambda: te.matmul_mx(T["ps%d" % bank][:, 0:n], T["q" + st][:, so:so + 128], T["s" + st][:, so:so + 128],
+                                       T["q" + mv][:, a:a + n], T["s" + mv][:, a:a + n], True, True), reads, ["ps%d" % bank])
+
+    def fill(ap, c, w):
+        emit("v", lambda: v.memset(ap, c), [], [w])
+
+    def iota(ap, pat, base, cm, w, ints=False):
+        if ints:
+            emit("g", lambda: g.iota(ap, pat, base, cm), [], [w])
+        else:
+            emit("g", lambda: g.iota(ap, pat, base, cm, allow_small_or_imprecise_dtypes=True), [], [w])
+
+    def aff(out, in_, pat, op, fillv, base, cm, reads, writes):
+        emit("g", lambda: g.affine_select(out, in_, pat, op, fillv, base, cm), reads, writes)
+
+    def dma(q, out, in_, reads, writes, sem):
+        emit(q, lambda: queue[q].dma_start(out, in_), reads, writes, sem, 16)
+
+    dma("sy", T.xt[:], T.x[:], [], ["xt"], "lx")
+    dma("a", T.ut[:], T.u[:], [], ["ut"], "lu")
+    dma("sy", u8(T.qw[:]), T.wc[:], [], ["qw"], "lw")
+    dma("sy", T.sw[:], T.ws[:], [], ["sw"], "lws")
+    dma("sy", T.vt[:], T.v[:], [], ["vt"], "lv")
+
+    names = []
+
+    def col(n):
+        if n not in names:
+            names.append(n)
+        i = names.index(n)
+        return T.pc[:, i:i + 1]
+
+    def cs(out, in0, s1, s2, op0, op1, *reads):
+        ts(col(out), col(in0), s1, s2, op0, op1, ["c." + x for x in (in0,) + reads], ["c." + out])
+
+    def floor_to(out, in_, step):
+        c = magic(step)
+        cs("tmp" + out, in_, -(step - 1) / 2.0, c, OP.add, OP.add)
+        cs(out, "tmp" + out, c, None, OP.subtract, None)
+
+    iota(col("p"), [[0, 1]], 0, 1, "c.p")
+    iota(T.ja[:], [[0, 4], [16, 2]], 0, 0, "ja")
+    iota(T.gm0[:], [[1, 1], [0, 128]], 0, 0, "gm0")
+    iota(T.m8[:], [[0, 16], [1, 8]], 0, 0, "m8", True)
+    iota(T.i3[:], [[4, 8], [0, 4], [1, 4]], 0, 0, "i3")
+    for t in range(4):
+        aff(T["ct%d" % t][:], T.i3[:], [[0, 8], [1, 4], [0, 4]], OP.is_equal, -1.0, -t, 0, ["i3"], ["ct%d" % t])
+    for l in range(1, 4):
+        iota(T["gm%d" % l][:], [[1, 2 ** l], [0, 128 >> l]], 0, 0, "gm%d" % l)
+    fill(T.st[:], 0.0, "st")
+    fill(T.zero[:], 0.0, "zero")
+    for n, w in (("fls", 680), ("flh", 544), ("idt", 520), ("ids", 520)):
+        act(T[n][:], T.zero[:, 0:w], ["zero"], [n])
+    iota(T.one[:], [[0, 128]], 1, 0, "one")
+    iota(T.d0a[:], [[64, 8], [1, 36]], -274, 0, "d0a")
+    aff(T.idt[:, 4:516:4], T.one[:], [[-1, 128]], OP.is_equal, 0.0, 0, 1, ["one", "idt"], ["idt"])
+    aff(T.ids[:, 4:516:4], T.one[:], [[-16, 4], [0, 2], [-1, 16]], OP.is_equal, 0.0, 0, 1, ["one", "ids"], ["ids"])
+    aff(T.ids[:, 4:68:4], T.one[:, 0:16], [[-1, 16]], OP.is_equal, 0.0, -112, 1, ["one", "ids"], ["ids"])
+    iota(T.j16[:], [[0, 18], [1, 16]], 0, 0, "j16")
+    iota(T.onef[:], [[0, C]], 1, 0, "onef")
+    aff(T.r16[:], T.onef[:], [[0, 18], [1, 16]], OP.not_equal, 0.0, 0, 0, ["onef"], ["r16"])
+    iota(T.own[:], [[1, C]], -144, 0, "own")
+    iota(T.j4[:], [[0, 72], [4, 4]], 0, 0, "j4")
+    aff(T.r4[:], T.onef[:], [[0, 72], [1, 4]], OP.not_equal, 0.0, 0, 0, ["onef"], ["r4"])
+    iota(T.jn[:], [[16, 18]], 0, 0, "jn")
+    iota(T.d0b[:], [[1, 36], [64, 8]], -274, 0, "d0b")
+
+    floor_to("q32", "p", 32)
+    floor_to("g16", "p", 16)
+    floor_to("p64", "p", 64)
+    cs("r", "q32", -1.0, col("p"), OP.mult, OP.add, "p")
+    cs("q", "g16", -1.0, col("p"), OP.mult, OP.add, "p")
+    cs("qb", "p64", -1.0, col("q32"), OP.mult, OP.add, "q32")
+    cs("g3", "r", 1.0 / 3.0, -1.0 / 3.0, OP.mult, OP.add)
+    ts(T.ja[:], T.ja[:], col("q"), None, OP.add, None, ["ja", "c.q"], ["ja"])
+    cs("G", "g3", magic(1), magic(1), OP.add, OP.subtract)
+    ts(T.jb[:], T.ja[:], 1.0 / 3.0, -1.0 / 3.0, OP.mult, OP.add, ["ja"], ["jb"])
+    cs("i", "G", -3.0, col("r"), OP.mult, OP.add, "r")
+    ts(T.jb[:], T.jb[:], magic(1), magic(1), OP.add, OP.subtract, ["jb"], ["jb"])
+    cs("i0", "i", 0.0, None, OP.is_equal, None)
+    ts(T.jb[:], T.jb[:], 13.0, None, OP.mult, None, ["jb"], ["jb"])
+    cs("wk0", "i0", 1.0, col("i"), OP.mult, OP.subtract, "i")
+    tt(T.jb[:], T.jb[:], T.ja[:], OP.add, ["jb", "ja"], ["jb"])
+    cs("wk", "wk0", 3.0, None, OP.add, None)
+    ts(T.ul[:], T.jb[:], 127.0, None, OP.min, None, ["jb"], ["ul"])
+    cs("v", "qb", 0.0, None, OP.is_equal, None)
+    cs("odd", "q32", -1.0, col("g16"), OP.mult, OP.add, "g16")
+    cs("a1", "p", 32.0, col("wk"), OP.is_lt, OP.mult, "wk")
+    cs("a2", "p", 64.0, col("i0"), OP.is_lt, OP.mult, "i0")
+    cs("a3", "p", 64.0, col("i0"), OP.is_ge, OP.mult, "i0")
+    cs("a4", "a1", 1.0, col("a2"), OP.mult, OP.add, "a2")
+    cs("wM", "a4", 1024.0, col("a3"), OP.mult, OP.add, "a3")
+
+    def const_m(l):
+        ts(T.st[:, 0:512:4], T["gm%d" % l][:], col("G"), col("wM"), OP.is_equal, OP.mult, ["gm%d" % l, "c.G", "c.wM", "st"], ["st"])
+        quant("m%d" % l, 0, 128, T.st[:], ["st"], ["qm%d" % l])
+
+    def const_p(l):
+        ts(T.eq[:], T["gm%d" % l][:], col("G"), None, OP.is_equal, None, ["gm%d" % l, "c.G"], ["eq"])
+        tt(T.st[:, 0:512:4], T.eq[:], T.xp[:], OP.mult, ["eq", "xp", "st"], ["st"])
+        quant("p%d" % l, 0, 128, T.st[:], ["st"], ["qp%d" % l])
+
+    quant("u0", 0, 128, T.ut[:], ["ut"], ["qu0"])
+    emit("v", lambda: v.tensor_copy(T.qu[:, 0:128].bitcast(dt.uint32), T.qu0[:, 0:128].bitcast(dt.uint32).indirect(T.ul[:, 0:8])), ["qu0", "ul"], ["qu"])
+    emit("a", lambda: s_.activation(T.su[:, 0:128], T.su0[:, 0:128].indirect(T.ul[:, 0:8]), CP), ["qu0", "ul"], ["su"])
+    quant("x", 0, NS, T.xt[:, 0:4 * NS], ["xt"], ["qxs"])
+    quant("x", NS, C, T.xt[:, 4 * NS:4 * C], ["xt"], ["qxh"])
+    const_m(0)
+    cs("G4", "G", 4.0, None, OP.mult, None)
+    cs("pw0", "i", 2.0, col("i"), OP.is_equal, OP.add, "i")
+    cs("R", "q32", 1.0 / 32.0, col("G4"), OP.mult, OP.add, "G4")
+    cs("pw", "pw0", 1.0, None, OP.add, None)
+    cs("v4", "v", 4.0, None, OP.mult, None)
+    cs("wP", "p", 64.0, BIG, OP.is_lt, OP.mult)
+    for t in range(4):
+        ts(T.kt3[:, t:512:4], T["ct%d" % t][:], col("R"), col("wk"), OP.is_equal, OP.mult, ["ct%d" % t, "c.R", "c.wk"], ["kt3.%d" % t])
+    k3 = ["kt3.%d" % t for t in range(4)]
+    for gg in range(8):
+        a = 64 * (gg // 2)
+        act(T.kt2[:, 64 * gg:64 * gg + 64], T.kt3[:, a:a + 64], k3, ["kt2.%d" % gg])
+    for h in range(4):
+        a = 128 * (h // 2)
+        act(T.kt1[:, 128 * h:128 * h + 128], T.kt2[:, a:a + 128], ["kt2.%d" % x for x in range(4)], ["kt1.%d" % h])
+
+    MAPS = [dict(d0="d0a", sl=lambda k: (36 * k, 36 * k + 36, 1), al=1.0, be=0.4375, ga=161.0),
+            dict(d0="d0b", sl=lambda k: (k, C, 8), al=8.0, be=7.984375, ga=140.0)]
+
+    def front(h):
+        f, n, o, w, b = ("flh", NH, 0, 512, 0) if h else ("fls", NS, 40, 0, 0)
+        S = T["ps%d" % b]
+        mm(b, n, "u", 0, "x", NS if h else 0, ["qu", "su", "qxh" if h else "qxs"])
+        F = T[f]
+        ts(F[:, o:o + 4 * n:4], S[:, 0:n], 0.0, col("v"), OP.is_gt, OP.is_equal, ["ps%d" % b, "c.v"], [f])
+        for Q in range(4):
+            ts(F[32 * Q:32 * Q + 32, w:w + n // 4], S[32 * Q:32 * Q + 32, Q:n:4], 0.0, None, OP.is_gt, None, ["ps%d" % b], [f + ".%d" % Q])
+        rds = [f] + [f + ".%d" % Q for Q in range(4)]
+        if h:
+            quant("f", 170, 306, F[:, 0:544], rds, ["qfh"])
+        else:
+            quant("f", 0, 170, F[:, 0:680], rds, ["qfs"])
+
+    def list_mm(l, h, bank):
+        if h:
+            mm(bank, 128, "k%d" % l, 0, "f", 178, ["qk%d" % l, "qfh"])
+        else:
+            mm(bank, 128, "k%d" % l, 0, "f", 0, ["qk%d" % l, "qfs"])
+
+    def list_out(l, h, bank):
+        a, b, i = (10, 18, 120) if h else (0, 10, 0)
+        ts(T["list%d" % l][:, a:b], T["ps%d" % bank][:, i:i + b - a], col("odd"), None, OP.add, None, ["ps%d" % bank, "c.odd"], ["list%d.%d" % (l, h)])
+
+    front(0)
+    ts(T.mb[:], T.m8[:], col("pw"), None, OP.mult, None, ["m8", "c.pw"], ["mb"])
+    ts(T.mc[:], T.mb[:], 4, None, OP.bitwise_and, None, ["mb"], ["mc"])
+    ts(T.xp[:], T.mc[:], col("v4"), col("wP"), OP.not_equal, OP.mult, ["mc", "c.v4", "c.wP"], ["xp"])
+    const_p(0)
+    for l in (3, 2, 1):
+        quant("k%d" % l, 0, 128, T["kt%d" % l][:], k3 if l == 3 else ["kt2.%d" % x for x in range(8)] if l == 2 else ["kt1.%d" % x for x in range(4)], ["qk%d" % l])
+
+    qx = ["qxs", "qxh"]
+    qf = ["qfs", "qfh"]
+    Tk = ["t.%d" % k for k in range(8)]
+    direct = topo.may_write(core, nxt)
+    hopmates = relays(topo, core, nxt)
+    indirect_in = relays(topo, prv, core)
+    sent = 0
+
+    for r in range(R):
+        mp = MAPS[0 if r == 0 else 1]
+        D0 = T[mp["d0"]]
+        view = lambda buf_, k: buf_[:, mp["sl"](k)[0]:mp["sl"](k)[1]:mp["sl"](k)[2]]
+        front(1)
+        if r == 0:
+            for l in (1, 2, 3):
+                list_mm(l, 0, l)
+            for l in (1, 2, 3):
+                list_out(l, 0, l)
+
+        def f_mm(j):
+            e = ("e%d" if j < 4 else "h%d") % (j % 4)
+            mm(6 + j % 2, C, e, 0, "x", 0, ["q" + e] + qx)
+
+        def f_out(j):
+            dst, key = (T.fh, "fh") if j < 4 else (T.fp, "fp")
+            act(dst[:, j % 4:4 * C:4], T["ps%d" % (6 + j % 2)][:, 0:C], ["ps%d" % (6 + j % 2)], [key + ".%d" % (j % 4)], scale=0.5)
+
+        def lev_mm(l, bank, pb):
+            mm(bank, C, "m%d" % l, 0, "f", 10, ["qm%d" % l] + qf)
+            if pb is not None:
+                mm(pb, C, "p%d" % l, 0, "f", 10, ["qp%d" % l] + qf)
+
+        if r > 0:
+            f_mm(0); f_out(0); f_mm(1); f_out(1)
+        lev_mm(0, 1, 2)
+        if r == 0:
+            const_m(1)
+            const_p(1)
+            cs("t1", "p", 64.0, THR, OP.is_ge, OP.mult)
+            cs("t2", "p", 32.0, THR, OP.is_ge, OP.mult)
+            cs("t3", "p", 16.0, THR, OP.is_ge, OP.mult)
+            fill(T.z32[:], 0.0, "z32")
+            for l in (1, 2, 3):
+                ts(T["thr%d" % l][:], T.z32[:], col("t%d" % l), None, OP.add, None, ["z32", "c.t%d" % l], ["thr%d" % l])
+        list_mm(1, 1, 3)
+        lev_mm(1, 4, 5)
+        list_mm(2, 1, 0)
+
+        def level(l, bank, pb):
+            d0, dk = (D0, mp["d0"]) if l == 0 else (T.wt, "wt")
+            for k in range(8):
+                scan(view(T.t, k), view(d0, k), view(T["ps%d" % bank], k), -1.0e6, OP.max, OP.add, [dk, "ps%d" % bank], [Tk[k]])
+            if l == 3:
+                return
+            x1, y1 = T.sm[:, 0:1], T.sm[:, 1:2]
+            tt(T.pv[:], T.t[:], T["ps%d" % pb][:, 0:C], OP.add, Tk + ["ps%d" % pb], ["pv"])
+            emit("v", lambda: v.tensor_reduce(x1, T.pv[:], AxisListType.X, OP.min), ["pv"], ["x1"])
+            list_out(l + 1, 1, {1: 3, 2: 0, 3: 3}[l + 1])
+            ts(y1, x1, magic(1024), magic(1024), OP.add, OP.subtract, ["x1"], ["y1"])
+            th = "thr%d" % (l + 1)
+            ts(T.bc[:], T[th][:], x1, y1, OP.is_gt, OP.mult, [th, "x1", "y1"], ["bc"])
+            emit("v", lambda: v.transpose(T.tr[:], T.bc[:]), ["bc"], ["tr"])
+            ll = ["list%d.0" % (l + 1), "list%d.1" % (l + 1)]
+            tt(T.wt[:], T.tr[:, 0:32].indirect(T["list%d" % (l + 1)][:, 0:18]), D0[:], OP.add, ["tr", mp["d0"]] + ll, ["wt"])
+
+        level(0, 1, 2)
+        if r > 0:
+            f_mm(2); f_out(2); f_mm(3); f_out(3)
+        if r == 0:
+            const_m(2)
+            const_p(2)
+            const_m(3)
+        list_mm(3, 1, 3)
+        lev_mm(2, 1, 2)
+        if r == 0:
+            for b in range(4):
+                quant("e%d" % b, 0, 128, T.idt[:, 4 - b:516 - b], ["idt"], ["qe%d" % b])
+                quant("h%d" % b, 0, 128, T.ids[:, 4 - b:516 - b], ["ids"], ["qh%d" % b])
+            for j in range(4):
+                f_mm(j); f_out(j)
+        f_mm(4); f_out(4); f_mm(5); f_out(5)
+        level(1, 4, 5)
+        lev_mm(3, 4, None)
+        f_mm(6); f_out(6); f_mm(7); f_out(7)
+        dma("sy", T.fp[:, 4 * C:8 * C], T.fp[:, 0:4 * C], ["fp.%d" % b for b in range(4)], ["fp2"], "fpd")
+        level(2, 1, 2)
+        if r == 0:
+            ts(T.mask16[:], T.j16[:], col("q"), -1.0, OP.is_equal, OP.mult, ["j16", "c.q"], ["mask16"])
+        level(3, 4, None)
+        for h in range(2):
+            c = slice(144 * h, 144 * h + 144)
+            tt(T.ex[:, c], T.t[:, c], T.mask16[:, c], OP.mult, Tk + ["mask16"], ["ex.%d" % h])
+            scan(T.scx[:, c], T.r16[:, c], T.ex[:, c], 0.0, OP.mult, OP.add, ["r16", "ex.%d" % h], ["scx.%d" % h])
+        for a in range(NA):
+            emit("a", lambda a=a: s_.activation(T.junk[:, C * a:C * a + C], T.t[:], ActivationFunctionType.Sign, bias=T.scx[:, 16 * a + 15:16 * a + 16],
+                                                accum_out=T.acc[:, a:a + 1]), Tk + ["scx.%d" % (a // 9)], ["acc.%d" % a])
+        if r == 0:
+            fill(T.r144[:], 1.0, "r144")
+            fill(T.r144[:, 0:C:144], 0.0, "r144")
+
+        def cmp_scan(j):
+            scan(T.cs[:, C * j:C * j + C], T.r144[:], T.cf[:, C * j:C * j + C], 0.0, OP.mult, OP.add, ["r144", "cf.%d" % j], ["cs.%d" % j])
+        for j in range(NV):
+            a = NA + j
+            ts(T.cf[:, C * j:C * j + C], T.t[:], T.scx[:, 16 * a + 15:16 * a + 16], 0.0, OP.add, OP.is_lt, Tk + ["scx.1"], ["cf.%d" % j])
+            if j > 0:
+                cmp_scan(j - 1)
+        x1, y1, lo, z, e1, e2, en = [T.sm[:, i:i + 1] for i in range(7)]
+        tt(lo, x1, y1, OP.subtract, ["x1", "y1"], ["lo"])
+        cmp_scan(NV - 1)
+        ts(z, lo, magic(64), magic(64), OP.add, OP.subtract, ["lo"], ["z"])
+        ts(e1, lo, 512.0 * mp["al"], 512.0 * (mp["ga"] + 288.0), OP.mult, OP.add, ["lo"], ["e1"])
+        tt(T.rkv[:], T.cs[:, 143:NV * C:288], T.cs[:, 287:NV * C:288], OP.add, ["cs.%d" % j for j in range(NV)], ["rkv"])
+        ts(e2, z, -512.0 * mp["be"], e1, OP.mult, OP.add, ["z", "e1"], ["e2"])
+        emit("v", lambda: v.tensor_copy(T.off[:, NA:18], T.rkv[:]), ["rkv"], ["off.v"])
+        ts(T.bcb[:], T.thr3[:], x1, e2, OP.is_gt, OP.mult, ["thr3", "x1", "e2"], ["bcb"])
+        emit("v", lambda: v.transpose(T.trb[:], T.bcb[:]), ["bcb"], ["trb"])
+        tt(T.val[:], T.trb[:, 0:32].indirect(T.list3[:, 0:18]), T.own[:], OP.add, ["trb", "own", "list3.0", "list3.1"], ["val"])
+        if r == 0:
+            floor_to("k4", "q", 4)
+            cs("e", "k4", -1.0, col("q"), OP.mult, OP.add, "q")
+            cs("eo", "e", 576.0, None, OP.add, None)
+            ts(T.mask4[:], T.j4[:], col("k4"), None, OP.is_equal, None, ["j4", "c.k4"], ["mask4"])
+        ts(T.off[:, 0:NA], T.acc[:], -0.5, 143.5, OP.mult, OP.add, ["acc.%d" % a for a in range(NA)], ["off.a"])
+        emit("v", lambda: v.tensor_copy(T.lin[:, 0:C].indirect(T.off[:, 0:18]), T.val[:]), ["off.a", "off.v", "val"], ["lin"])
+        tt(T.ml[:, 0:K], T.lin[:, 0:K], T.mask4[:, 0:K], OP.mult, ["lin", "mask4"], ["ml.0"])
+        scan(T.sc[:, 0:K], T.r4[:, 0:K], T.ml[:, 0:K], 0.0, OP.mult, OP.add, ["r4", "ml.0"], ["sc.0"])
+        W = T.sc[:, 3:K:4]
+        ts(T.ta[:, 0:32], W, magic(512), magic(512), OP.add, OP.subtract, ["sc.0"], ["ta"])
+        tt(T.oa[:, 0:32], W, T.ta[:, 0:32], OP.subtract, ["sc.0", "ta"], ["oa"])
+        ts(T.lu[:], T.oa[:, 0:32], 4.0, col("eo"), OP.mult, OP.add, ["oa", "c.eo"], ["lu"])
+        fhk = ["fh.%d" % b for b in range(4)]
+        for h in range(2):
+            act(T.g1[:, 256 * h:256 * h + 256], T.fh[:, 0:4 * C].indirect(T.lu[:, 16 * h:16 * h + 16]), fhk + ["lu"], ["g1.%d" % h])
+        ts(T.la[:], T.oa[:, 0:32], 4.0, col("eo"), OP.mult, OP.add, ["oa", "c.eo"], ["la"])
+        ts(T.lb[:], T.ta[:, 0:32], 1.0 / 128.0, col("e"), OP.mult, OP.add, ["ta", "c.e"], ["lb"])
+        tt(T.lb[:], T.lb[:], T.la[:], OP.max, ["lb", "la"], ["lb"])
+        emit("v", lambda: v.tensor_copy(T.bu[:], T.lb[:]), ["lb"], ["bu"])
+        for h in range(2):
+            tt(T.zt[:, 256 * h:256 * h + 256], T.fp[:, 0:8 * C].indirect(T.bu[:, 16 * h:16 * h + 16]), T.g1[:, 256 * h:256 * h + 256], OP.add,
+               ["fp.%d" % b for b in range(4)] + ["fp2", "bu", "g1.%d" % h], ["zt.%d" % h])
+        quant("z", K * r, K * r + K, T.zt[:], ["zt.0", "zt.1"], ["qz%d" % r])
+
+        def send():
+            tr = []
+            sem = T.sem[("arr%d" if direct else "rar%d") % r]
+            for j in range(4):
+                d = nxt if direct else hopmates[j]
+                es = topo.engines(core, d)
+                rid, pid = topo.addr(d, core)
+                dst = T.qa[:, K * r + 32 * j:K * r + 32 * j + 32] if direct else T.rq[:, 32 * r:32 * r + 32]
+                tr.append(RemoteDMATransfer(dst_ids=[DstId(rid=rid, pnc=pid)], dma_engine_mask=bits(es[2 * j:2 * j + 2]),
+                                            remote_sem=sem, src=u8(T.qz[:, K * r + 32 * j:K * r + 32 * j + 32]), dst=u8(dst)))
+            d = nxt if direct else hopmates[0]
+            es = topo.engines(core, d)
+            rid, pid = topo.addr(d, core)
+            tr.append(RemoteDMATransfer(dst_ids=[DstId(rid=rid, pnc=pid)], dma_engine_mask=bits(es[len(es) // 2:]),
+                                        remote_sem=sem, src=T.sz[:, K * r:K * r + K], dst=(T.sa if direct else T.rs)[:, K * r:K * r + K]))
+            g.remote_dma_fused(tr, local_sem=T.sem.snt)
+            return 8 + len(es) // 2
+        cnt = [0]
+
+        def do_send():
+            cnt[0] = send()
+        emit("g", do_send, ["qz%d" % r], [])
+        sent += cnt[0]
+
+        tt(T.ml[:, K:C], T.lin[:, K:C], T.mask4[:, K:C], OP.mult, ["lin", "mask4"], ["ml.1"])
+        scan(T.sc[:, K:C], T.r4[:, K:C], T.ml[:, K:C], 0.0, OP.mult, OP.add, ["r4", "ml.1"], ["sc.1"])
+        W2 = T.sc[:, K + 3:C:4]
+        ts(T.tsv[:], W2, magic(512), magic(512), OP.add, OP.subtract, ["sc.1"], ["tsv"])
+        tt(T.osv[:], W2, T.tsv[:], OP.subtract, ["sc.1", "tsv"], ["osv"])
+        ts(T.sul[:], T.osv[:], 4.0, col("eo"), OP.mult, OP.add, ["osv", "c.eo"], ["sul"])
+        act(T.xs[:], T.fh[:, 0:4 * C].indirect(T.sul[:, 0:40]), fhk + ["sul"], ["xs"], scale=2.0)
+        if r == R - 1:
+            ts(T.o1[:], T.lin[:], magic(512), magic(512), OP.add, OP.subtract, ["lin"], ["o1"])
+            tt(T.o2[:], T.lin[:], T.o1[:], OP.subtract, ["lin", "o1"], ["o2"])
+        quant("x", 0, NS, T.xs[:], ["xs"], ["qxs"])
+        if r < R - 1:
+            front(0)
+            for l in (1, 2, 3):
+                list_mm(l, 0, l)
+            for l in (1, 2, 3):
+                list_out(l, 0, l)
+        else:
+            ts(T.jn[:], T.jn[:], col("q"), None, OP.add, None, ["jn", "c.q"], ["jn"])
+            ts(T.jk[:], T.jn[:], 1.0 / 36.0, -17.5 / 36.0, OP.mult, OP.add, ["jn"], ["jk"])
+            ts(T.jk[:], T.jk[:], magic(1), magic(1), OP.add, OP.subtract, ["jk"], ["jk"])
+            ts(T.jk[:], T.jk[:], -287.0, None, OP.mult, None, ["jk"], ["jk"])
+            ts(T.jn[:], T.jn[:], 8.0, None, OP.mult, None, ["jn"], ["jn"])
+            tt(T.jn[:], T.jn[:], T.jk[:], OP.add, ["jn", "jk"], ["jn"])
+            emit("v", lambda: v.tensor_copy(T.nat[:], T.jn[:]), ["jn"], ["nat"])
+            quant("v", 0, 128, T.vt[:], ["vt"], ["qv"])
+            ts(T.o3[:], T.o2[:], 140.5, magic(8), OP.add, OP.add, ["o2"], ["o3"])
+            ts(T.o1[:], T.o2[:], 36.0, 5184.0, OP.mult, OP.add, ["o2"], ["o1"])
+            ts(T.o4[:], T.o3[:], magic(8), -35.875, OP.subtract, OP.mult, ["o3"], ["o4"])
+            tt(T.opt[:], T.o1[:], T.o4[:], OP.add, ["o1", "o4"], ["opt"])
+            dma("sy", T.op[:], T.opt[0:128:16, :], ["opt"], [], "od")
+
+        ne = 4 * 4 + 4 if indirect_in else 8 + len(topo.engines(prv, core)) // 2
+        g.tensor.wait_ge(T.sem["arr%d" % r], ne)
+        for b in range(4):
+            mm(b, K, "w", 128 * b, "a", K * r, ["qw", "sw"])
+            act(T.tm[:, K * b:K * b + K], T["ps%d" % b][:, 0:K], ["ps%d" % b], ["tm.%d" % b], scale=0.0078125)
+            mm(4 + b, K, "e%d" % b, 0, "a", K * r, ["qe%d" % b])
+            tt(T.xh[:, b:512:4], T.tm[:, K * b:K * b + K], T["ps%d" % (4 + b)][:, 0:K], OP.add, ["tm.%d" % b, "ps%d" % (4 + b)], ["xh.%d" % b])
+        quant("x", NS, C, T.xh[:], ["xh.%d" % b for b in range(4)], ["qxh"])
+
+    emit("v", lambda: v.tensor_copy(T.qn[:, 0:C].bitcast(dt.uint32), T.qx[:, 0:C].bitcast(dt.uint32).indirect(T.nat[:, 0:18])), qx + ["nat"], ["qn"])
+    emit("a", lambda: s_.activation(T.sn[:, 0:C], T.sx[:, 0:C].indirect(T.nat[:, 0:18]), CP), qx + ["nat"], ["sn"])
+    mm(0, C, "v", 0, "n", 0, ["qv", "qn", "sn"])
+    dma("sy", T.oc[:], u8(T.qn[:]), ["qn"], [], "od")
+    for k in range(4):
+        dma("a", T.osc[4 * k:4 * k + 4, :], T.sn[32 * k:32 * k + 4, :], ["sn"], [], "od")
+    emit("v", lambda: v.tensor_copy(T.yt[:], T.ps0[:, 0:C]), ["ps0"], ["yt"])
+    dma("sy", T.y[:], T.yt[:], ["yt"], [], "od")
+    for s in count:
+        g.wait_ge(T.sem[s], count[s])
+    g.wait_ge(T.sem.snt, sent)

@@ -2,8 +2,10 @@ from concourse.bass import DstId, RemoteDMATransfer
 from concourse.mybir import dt, AluOpType, AxisListType, ActivationFunctionType
 
 OP = AluOpType
-CP = ActivationFunctionType.Copy
+AF = ActivationFunctionType
+CP = AF.Copy
 C, K, R, NS, NH = 288, 128, 3, 160, 128
+SOURCE = [7, 0, 1, 1, 2, 2, 3, 3]
 NA = 13
 NV = 18 - NA
 THR = 1572864.0
@@ -33,25 +35,24 @@ for _b in range(8):
     buf("ps%d" % _b, 512, "float32", "psum")
 buf("xt", 4 * C, "bfloat16"); buf("ut", 512, "bfloat16"); buf("vt", 512, "bfloat16")
 pair("u0", 128); pair("u", 128); pair("v", 128); pair("w", 512); pair("x", C); pair("n", C); pair("f", 306)
-CONST = {n: 128 * i for i, n in enumerate(["m0", "m1", "m2", "m3", "p0", "p1", "p2", "k1", "k2", "k3",
-                                           "e0", "e1", "e2", "e3", "h0", "h1", "h2", "h3"])}
+CONST = {n: 128 * i for i, n in enumerate(["m0", "m1", "m2", "m3", "p0", "p1", "p2", "k1", "k2", "k3", "e0", "e1", "e2", "e3"])}
 pair("k", 128 * len(CONST))
 for _l in (1, 2, 3):
     buf("kt%d" % _l, 512, "bfloat16")
     buf("list%d" % _l, 18, "uint16")
     buf("thr%d" % _l, 32)
 pair("z", R * K); pair("a", R * K)
-buf("rq", 32 * R, CODE); buf("rs", K * R, "uint8")
-buf("pc", 64); buf("st", 512, "bfloat16"); buf("zero", 680, "bfloat16")
+buf("rq", 64 * R, CODE); buf("rs", K * R, "uint8")
+buf("pc", 64); buf("pi", 8, "int32"); buf("ab", 128); buf("st", 512, "bfloat16"); buf("zero", 680, "bfloat16")
 buf("gm0", 128); buf("gm1", 128); buf("gm2", 128); buf("gm3", 128)
 buf("m8", 128, "int32"); buf("mb", 128, "int32"); buf("mc", 128, "int32"); buf("xp", 128); buf("eq", 128)
 buf("i3", 128)
 for _t in range(4):
     buf("ct%d" % _t, 128)
-buf("one", 128, "bfloat16"); buf("idt", 520, "bfloat16"); buf("ids", 520, "bfloat16")
+buf("one", 128, "bfloat16"); buf("idt", 520, "bfloat16")
 buf("onef", C); buf("j16", C); buf("j4", C); buf("mask16", C); buf("mask4", C); buf("r16", C); buf("r4", C)
 buf("r144", C, "bfloat16")
-buf("d0a", C); buf("d0b", C); buf("own", C); buf("z32", 32)
+buf("zf", C); buf("d0a", C); buf("d0b", C); buf("own", C); buf("z32", 32)
 buf("jn", 18); buf("jk", 18); buf("nat", 18, "uint16")
 buf("ja", 8); buf("jb", 8); buf("ul", 8, "uint16")
 buf("fls", 680, "bfloat16"); buf("flh", 544, "bfloat16")
@@ -63,7 +64,7 @@ buf("ta", 40); buf("oa", 40); buf("la", 32); buf("lb", 32); buf("lu", 32, "uint1
 buf("tsv", 40); buf("osv", 40); buf("sul", 40, "uint16")
 buf("fh", 4 * C, "bfloat16"); buf("fp", 8 * C, "bfloat16")
 buf("g1", 512); buf("zt", 512, "bfloat16"); buf("xs", 640, "bfloat16"); buf("xh", 512, "bfloat16")
-buf("tm", 512); buf("o1", C); buf("o2", C); buf("o3", C); buf("o4", C); buf("opt", C); buf("yt", C)
+buf("o1", C); buf("o2", C); buf("o3", C); buf("o4", C); buf("opt", C); buf("yt", C)
 
 SEMAPHORES = ["ev", "ea", "ep", "eg", "lx", "lu", "lw", "lws", "lv", "fpd", "od", "snt"]
 SEMAPHORES += ["arr%d" % _r for _r in range(R)] + ["rar%d" % _r for _r in range(R)]
@@ -72,7 +73,9 @@ SEMAPHORES += ["arr%d" % _r for _r in range(R)] + ["rar%d" % _r for _r in range(
 def relays(topo, a, b):
     if topo.may_write(a, b):
         return []
-    return [c for c in topo.cores_of(a) if c != a and topo.may_write(c, b)]
+    own = [c for c in topo.cores_of(a) if c != a and topo.may_write(c, b)]
+    other = [c for c in own if topo.die(c) != topo.die(own[0])]
+    return [own[0], other[0], [c for c in own if c not in (own[0], other[0])][0]]
 
 
 def bits(es):
@@ -83,6 +86,11 @@ def u8(ap):
     return ap.bitcast(dt.uint8)
 
 
+def move(topo, src, dst, es, sem, out, in_):
+    rid, pid = topo.addr(dst, src)
+    return RemoteDMATransfer(dst_ids=[DstId(rid=rid, pnc=pid)], dma_engine_mask=bits(es), remote_sem=sem, src=in_, dst=out)
+
+
 def relay_program(g, core, T, topo):
     for i, a in enumerate(T.cores):
         b = T.cores[(i + 1) % len(T.cores)]
@@ -90,20 +98,16 @@ def relay_program(g, core, T, topo):
         if core not in rl:
             continue
         j = rl.index(core)
-        hop = topo.engines(a, core)
-        rid, pid = topo.addr(b, core)
         es = topo.engines(core, b)
-        total = 0
         for r in range(R):
-            g.wait_ge(T.sem["rar%d" % r], 2 + (len(hop) // 2 if j == 0 else 0))
-            tr = [RemoteDMATransfer(dst_ids=[DstId(rid=rid, pnc=pid)], dma_engine_mask=bits(es[::2]), remote_sem=T.sem["arr%d" % r],
-                                    src=u8(T.rq[:, 32 * r:32 * r + 32]), dst=u8(T.qa[:, K * r + 32 * j:K * r + 32 * j + 32]))]
-            if j == 0:
-                tr.append(RemoteDMATransfer(dst_ids=[DstId(rid=rid, pnc=pid)], dma_engine_mask=bits(es[1::2]), remote_sem=T.sem["arr%d" % r],
-                                            src=T.rs[:, K * r:K * r + K], dst=T.sa[:, K * r:K * r + K]))
-            g.remote_dma_fused(tr, local_sem=T.sem.snt)
-            total += len(es) // 2 * len(tr)
-        g.wait_ge(T.sem.snt, total)
+            if j < 2:
+                n, o = len(topo.engines(a, core)) // 2, K * r + 64 * j
+                out, in_ = u8(T.qa[:, o:o + 64]), u8(T.rq[:, 64 * r:64 * r + 64])
+            else:
+                n, out, in_ = len(topo.engines(a, core)), T.sa[:, K * r:K * r + K], T.rs[:, K * r:K * r + K]
+            g.wait_ge(T.sem["rar%d" % r], n)
+            g.remote_dma_fused([move(topo, core, b, es, T.sem["arr%d" % r], out, in_)], local_sem=T.sem.snt)
+        g.wait_ge(T.sem.snt, R * len(es))
 
 
 def rank_program(g, core, T, topo):
@@ -118,7 +122,7 @@ def rank_program(g, core, T, topo):
     known = {q: {} for q in queue}
     wr, rd = {}, {}
 
-    def emit(q, fn, reads, writes, sem=None, inc=1):
+    def emit(q, fn, reads, writes, sem=None, inc=1, acc=False):
         sem = sem or "e" + q
         need = {}
 
@@ -133,7 +137,8 @@ def rank_program(g, core, T, topo):
                         dep(d)
         for k in writes:
             for d in wr.get(k, []) + rd.get(k, []):
-                dep(d)
+                if not (acc and d[0] == q):
+                    dep(d)
         for s in need:
             if known[q].get(s, 0) < need[s]:
                 queue[q].wait_ge(T.sem[s], need[s])
@@ -172,11 +177,11 @@ def rank_program(g, core, T, topo):
     def act(out, in_, reads, writes, scale=1.0):
         emit("a", lambda: s_.activation(out, in_, CP, scale=scale), reads, writes)
 
-    def mm(bank, n, st, so, mv, a, reads):
+    def mm(bank, n, st, so, mv, a, reads, start=True, stop=True):
         if st in CONST:
             so, st = CONST[st], "k"
         emit("p", lambda: te.matmul_mx(T["ps%d" % bank][:, 0:n], T["q" + st][:, so:so + 128], T["s" + st][:, so:so + 128],
-                                       T["q" + mv][:, a:a + n], T["s" + mv][:, a:a + n], True, True), reads, ["ps%d" % bank])
+                                       T["q" + mv][:, a:a + n], T["s" + mv][:, a:a + n], start, stop), reads, ["ps%d" % bank], acc=not start)
 
     def fill(ap, c, w):
         emit("v", lambda: v.memset(ap, c), [], [w])
@@ -190,8 +195,8 @@ def rank_program(g, core, T, topo):
     def aff(out, in_, pat, op, fillv, base, cm, reads, writes):
         emit("g", lambda: g.affine_select(out, in_, pat, op, fillv, base, cm), reads, writes)
 
-    def dma(q, out, in_, reads, writes, sem):
-        emit(q, lambda: queue[q].dma_start(out, in_), reads, writes, sem, 16)
+    def dma(q, out, in_, reads, writes, sem, acc=False):
+        emit(q, lambda: queue[q].dma_start(out, in_), reads, writes, sem, 16, acc)
 
     dma("sy", T.xt[:], T.x[:], [], ["xt"], "lx")
     dma("a", T.ut[:], T.u[:], [], ["ut"], "lu")
@@ -210,11 +215,7 @@ def rank_program(g, core, T, topo):
     def cs(out, in0, s1, s2, op0, op1, *reads):
         ts(col(out), col(in0), s1, s2, op0, op1, ["c." + x for x in (in0,) + reads], ["c." + out])
 
-    def floor_to(out, in_, step):
-        c = magic(step)
-        cs("tmp" + out, in_, -(step - 1) / 2.0, c, OP.add, OP.add)
-        cs(out, "tmp" + out, c, None, OP.subtract, None)
-
+    iota(T.pi[:, 0:1], [[0, 1]], 0, 1, "pi", True)
     iota(col("p"), [[0, 1]], 0, 1, "c.p")
     iota(T.ja[:], [[0, 4], [16, 2]], 0, 0, "ja")
     iota(T.gm0[:], [[1, 1], [0, 128]], 0, 0, "gm0")
@@ -226,28 +227,32 @@ def rank_program(g, core, T, topo):
         iota(T["gm%d" % l][:], [[1, 2 ** l], [0, 128 >> l]], 0, 0, "gm%d" % l)
     fill(T.st[:], 0.0, "st")
     fill(T.zero[:], 0.0, "zero")
-    for n, w in (("fls", 680), ("flh", 544), ("idt", 520), ("ids", 520)):
+    for n, w in (("fls", 680), ("flh", 544), ("idt", 520)):
         act(T[n][:], T.zero[:, 0:w], ["zero"], [n])
-    iota(T.one[:], [[0, 128]], 1, 0, "one")
-    iota(T.d0a[:], [[64, 8], [1, 36]], -274, 0, "d0a")
+    iota(T.zf[:], [[0, C]], 0, 0, "zf")
+    iota(T.z32[:], [[0, 32]], int(THR), 0, "z32")
+    for l in (1, 2, 3):
+        aff(T["thr%d" % l][:], T.z32[:], [[0, 32]], OP.is_ge, 0.0, -(128 >> l), 1, ["z32"], ["thr%d" % l])
+    iota(T.one[:], [[0, 128]], 128, 0, "one")
     aff(T.idt[:, 4:516:4], T.one[:], [[-1, 128]], OP.is_equal, 0.0, 0, 1, ["one", "idt"], ["idt"])
-    aff(T.ids[:, 4:516:4], T.one[:], [[-16, 4], [0, 2], [-1, 16]], OP.is_equal, 0.0, 0, 1, ["one", "ids"], ["ids"])
-    aff(T.ids[:, 4:68:4], T.one[:, 0:16], [[-1, 16]], OP.is_equal, 0.0, -112, 1, ["one", "ids"], ["ids"])
+    iota(T.d0a[:], [[64, 8], [1, 36]], -274, 0, "d0a")
     iota(T.j16[:], [[0, 18], [1, 16]], 0, 0, "j16")
     iota(T.onef[:], [[0, C]], 1, 0, "onef")
     aff(T.r16[:], T.onef[:], [[0, 18], [1, 16]], OP.not_equal, 0.0, 0, 0, ["onef"], ["r16"])
+    iota(T.r144[:], [[0, C]], 1, 0, "r144")
+    aff(T.r144[:], T.r144[:], [[0, 2], [1, 144]], OP.not_equal, 0.0, 0, 0, ["r144"], ["r144"])
     iota(T.own[:], [[1, C]], -144, 0, "own")
     iota(T.j4[:], [[0, 72], [4, 4]], 0, 0, "j4")
     aff(T.r4[:], T.onef[:], [[0, 72], [1, 4]], OP.not_equal, 0.0, 0, 0, ["onef"], ["r4"])
     iota(T.jn[:], [[16, 18]], 0, 0, "jn")
     iota(T.d0b[:], [[1, 36], [64, 8]], -274, 0, "d0b")
 
-    floor_to("q32", "p", 32)
-    floor_to("g16", "p", 16)
-    floor_to("p64", "p", 64)
-    cs("r", "q32", -1.0, col("p"), OP.mult, OP.add, "p")
-    cs("q", "g16", -1.0, col("p"), OP.mult, OP.add, "p")
-    cs("qb", "p64", -1.0, col("q32"), OP.mult, OP.add, "q32")
+    low = [("r", 31), ("q", 15), ("q32", 96), ("odd", 16), ("k4", 12), ("e", 3), ("qb", 32)]
+    for n, m in low:
+        col(n)
+    for j, (n, m) in enumerate(low):
+        ts(T.pi[:, j + 1:j + 2], T.pi[:, 0:1], m, None, OP.bitwise_and, None, ["pi"], ["pi.%d" % j])
+    emit("v", lambda: v.tensor_copy(T.pc[:, 1:8], T.pi[:, 1:8]), ["pi.%d" % j for j in range(7)], ["c." + n for n, m in low])
     cs("g3", "r", 1.0 / 3.0, -1.0 / 3.0, OP.mult, OP.add)
     ts(T.ja[:], T.ja[:], col("q"), None, OP.add, None, ["ja", "c.q"], ["ja"])
     cs("G", "g3", magic(1), magic(1), OP.add, OP.subtract)
@@ -261,15 +266,23 @@ def rank_program(g, core, T, topo):
     cs("wk", "wk0", 3.0, None, OP.add, None)
     ts(T.ul[:], T.jb[:], 127.0, None, OP.min, None, ["jb"], ["ul"])
     cs("v", "qb", 0.0, None, OP.is_equal, None)
-    cs("odd", "q32", -1.0, col("g16"), OP.mult, OP.add, "g16")
     cs("a1", "p", 32.0, col("wk"), OP.is_lt, OP.mult, "wk")
     cs("a2", "p", 64.0, col("i0"), OP.is_lt, OP.mult, "i0")
     cs("a3", "p", 64.0, col("i0"), OP.is_ge, OP.mult, "i0")
     cs("a4", "a1", 1.0, col("a2"), OP.mult, OP.add, "a2")
-    cs("wM", "a4", 1024.0, col("a3"), OP.mult, OP.add, "a3")
+    cs("wM0", "a4", 1024.0, None, OP.mult, None)
+    cs("wM1", "a4", 1024.0, col("a3"), OP.mult, OP.add, "a3")
+
+    def hit(out, in_, c, w, reads, writes):
+        emit("a", lambda: s_.activation(T.ab[:], in_, AF.Abs, bias=col(c), scale=-1.0), reads + ["c." + c], ["ab"])
+        emit("a", lambda: s_.activation(out, T.ab[:], AF.Relu, bias=col(w), scale=col("n" + w)), ["ab", "c." + w, "c.n" + w], writes)
+
+    for w in ("wM0", "wM1", "wk"):
+        cs("n" + w, w, -1.0, None, OP.mult, None)
 
     def const_m(l):
-        ts(T.st[:, 0:512:4], T["gm%d" % l][:], col("G"), col("wM"), OP.is_equal, OP.mult, ["gm%d" % l, "c.G", "c.wM", "st"], ["st"])
+        w = "wM%d" % (l // 2)
+        hit(T.st[:, 0:512:4], T["gm%d" % l][:], "G", w, ["gm%d" % l, "st"], ["st"])
         quant("m%d" % l, 0, 128, T.st[:], ["st"], ["qm%d" % l])
 
     def const_p(l):
@@ -290,7 +303,7 @@ def rank_program(g, core, T, topo):
     cs("v4", "v", 4.0, None, OP.mult, None)
     cs("wP", "p", 64.0, BIG, OP.is_lt, OP.mult)
     for t in range(4):
-        ts(T.kt3[:, t:512:4], T["ct%d" % t][:], col("R"), col("wk"), OP.is_equal, OP.mult, ["ct%d" % t, "c.R", "c.wk"], ["kt3.%d" % t])
+        hit(T.kt3[:, t:512:4], T["ct%d" % t][:], "R", "wk", ["ct%d" % t], ["kt3.%d" % t])
     k3 = ["kt3.%d" % t for t in range(4)]
     for gg in range(8):
         a = 64 * (gg // 2)
@@ -340,7 +353,9 @@ def rank_program(g, core, T, topo):
     direct = topo.may_write(core, nxt)
     hopmates = relays(topo, core, nxt)
     indirect_in = relays(topo, prv, core)
-    sent = 0
+    fhk = ["fh.%d" % b for b in range(4)]
+    fpk = ["fp.%d" % x for x in range(16)]
+    sent = []
 
     for r in range(R):
         mp = MAPS[0 if r == 0 else 1]
@@ -353,56 +368,65 @@ def rank_program(g, core, T, topo):
             for l in (1, 2, 3):
                 list_out(l, 0, l)
 
-        def f_mm(j):
-            e = ("e%d" if j < 4 else "h%d") % (j % 4)
-            mm(6 + j % 2, C, e, 0, "x", 0, ["q" + e] + qx)
-
-        def f_out(j):
-            dst, key = (T.fh, "fh") if j < 4 else (T.fp, "fp")
-            act(dst[:, j % 4:4 * C:4], T["ps%d" % (6 + j % 2)][:, 0:C], ["ps%d" % (6 + j % 2)], [key + ".%d" % (j % 4)], scale=0.5)
+        def unpack(j):
+            mm(6 + j % 2, C, "e%d" % j, 0, "x", 0, ["qe%d" % j] + qx)
+            act(T.fh[:, j:4 * C:4], T["ps%d" % (6 + j % 2)][:, 0:C], ["ps%d" % (6 + j % 2)], ["fh.%d" % j], scale=0.5 / 128)
 
         def lev_mm(l, bank, pb):
             mm(bank, C, "m%d" % l, 0, "f", 10, ["qm%d" % l] + qf)
             if pb is not None:
                 mm(pb, C, "p%d" % l, 0, "f", 10, ["qp%d" % l] + qf)
 
-        if r > 0:
-            f_mm(0); f_out(0); f_mm(1); f_out(1)
-        lev_mm(0, 1, 2)
         if r == 0:
+            lev_mm(0, 1, 2)
             const_m(1)
             const_p(1)
-            cs("t1", "p", 64.0, THR, OP.is_ge, OP.mult)
-            cs("t2", "p", 32.0, THR, OP.is_ge, OP.mult)
-            cs("t3", "p", 16.0, THR, OP.is_ge, OP.mult)
-            fill(T.z32[:], 0.0, "z32")
-            for l in (1, 2, 3):
-                ts(T["thr%d" % l][:], T.z32[:], col("t%d" % l), None, OP.add, None, ["z32", "c.t%d" % l], ["thr%d" % l])
+        else:
+            unpack(0)
+            unpack(1)
+            mm(1, NH, "m0", 0, "f", 170, ["qm0", "qfh"])
+            mm(2, NH, "p0", 0, "f", 170, ["qp0", "qfh"])
         list_mm(1, 1, 3)
         lev_mm(1, 4, 5)
         list_mm(2, 1, 0)
 
         def level(l, bank, pb):
-            d0, dk = (D0, mp["d0"]) if l == 0 else (T.wt, "wt")
-            for k in range(8):
-                scan(view(T.t, k), view(d0, k), view(T["ps%d" % bank], k), -1.0e6, OP.max, OP.add, [dk, "ps%d" % bank], [Tk[k]])
-            if l == 3:
-                return
-            x1, y1 = T.sm[:, 0:1], T.sm[:, 1:2]
-            tt(T.pv[:], T.t[:], T["ps%d" % pb][:, 0:C], OP.add, Tk + ["ps%d" % pb], ["pv"])
-            emit("v", lambda: v.tensor_reduce(x1, T.pv[:], AxisListType.X, OP.min), ["pv"], ["x1"])
-            list_out(l + 1, 1, {1: 3, 2: 0, 3: 3}[l + 1])
-            ts(y1, x1, magic(1024), magic(1024), OP.add, OP.subtract, ["x1"], ["y1"])
-            th = "thr%d" % (l + 1)
-            ts(T.bc[:], T[th][:], x1, y1, OP.is_gt, OP.mult, [th, "x1", "y1"], ["bc"])
+            x1, y1, xs, xh = T.sm[:, 0:1], T.sm[:, 1:2], T.sm[:, 8:9], T.sm[:, 9:10]
+            B, P = T["ps%d" % bank], T["ps%d" % pb] if l < 3 else None
+            if l == 0 and r > 0:
+                for k in range(8):
+                    scan(T.t[:, NS + k:C:8], T.zf[:, NS + k:C:8], B[:, k:NH:8], T.t[:, NS - 8 + k:NS - 7 + k], OP.max, OP.add, ["zf", "ps%d" % bank, Tk[k]], ["th.%d" % k])
+                tt(T.pv[:, NS:C], T.t[:, NS:C], P[:, 0:NH], OP.add, ["th.%d" % k for k in range(8)] + ["ps%d" % pb], ["pv"])
+                emit("v", lambda: v.tensor_reduce(xh, T.pv[:, NS:C], AxisListType.X, OP.min), ["pv"], ["xh1"])
+                list_out(1, 1, 3)
+                tt(x1, xh, xs, OP.min, ["xh1", "xs1"], ["x1"])
+            else:
+                d0, dk = (T.zf, "zf") if l == 0 else (T.wt, "wt")
+                for k in range(8):
+                    scan(view(T.t, k), view(d0, k), view(B, k), -1.0e6, OP.max, OP.add, [dk, "ps%d" % bank], [Tk[k], "th.%d" % k])
+                if l == 3:
+                    return
+                tt(T.pv[:], T.t[:], P[:, 0:C], OP.add, Tk + ["ps%d" % pb], ["pv", "pvs"])
+                emit("v", lambda: v.tensor_reduce(x1, T.pv[:], AxisListType.X, OP.min), ["pv"], ["x1"])
+                list_out(l + 1, 1, {1: 3, 2: 0, 3: 3}[l + 1])
+            th, w = "thr%d" % (l + 1), x1
+            if l == 2:
+                ts(y1, x1, magic(1024), magic(1024), OP.add, OP.subtract, ["x1"], ["y1"])
+                w = y1
+            ts(T.bc[:], T[th][:], x1, w, OP.is_gt, OP.mult, [th, "x1", "y1"], ["bc"])
             emit("v", lambda: v.transpose(T.tr[:], T.bc[:]), ["bc"], ["tr"])
-            ll = ["list%d.0" % (l + 1), "list%d.1" % (l + 1)]
-            tt(T.wt[:], T.tr[:, 0:32].indirect(T["list%d" % (l + 1)][:, 0:18]), D0[:], OP.add, ["tr", mp["d0"]] + ll, ["wt"])
+            win = T.tr[:, 0:32].indirect(T["list%d" % (l + 1)][:, 0:18])
+            ll = ["tr", "list%d.0" % (l + 1), "list%d.1" % (l + 1)]
+            if l == 0:
+                emit("v", lambda: v.tensor_copy(T.wt[:], win), ll, ["wt"])
+            else:
+                tt(T.wt[:], win, D0[:], OP.add, [mp["d0"]] + ll, ["wt"])
 
         level(0, 1, 2)
         if r > 0:
-            f_mm(2); f_out(2); f_mm(3); f_out(3)
-        if r == 0:
+            unpack(2)
+            unpack(3)
+        else:
             const_m(2)
             const_p(2)
             const_m(3)
@@ -411,14 +435,14 @@ def rank_program(g, core, T, topo):
         if r == 0:
             for b in range(4):
                 quant("e%d" % b, 0, 128, T.idt[:, 4 - b:516 - b], ["idt"], ["qe%d" % b])
-                quant("h%d" % b, 0, 128, T.ids[:, 4 - b:516 - b], ["ids"], ["qh%d" % b])
             for j in range(4):
-                f_mm(j); f_out(j)
-        f_mm(4); f_out(4); f_mm(5); f_out(5)
+                unpack(j)
+        for h in range(2):
+            for gg in range(8):
+                e = 16 * SOURCE[gg]
+                dma("sy", T.fp[16 * gg:16 * gg + 16, 4 * C * h:4 * C * h + 4 * C], T.fh[e:e + 16, :], fhk, ["fp.%d" % (8 * h + gg)], "fpd", True)
         level(1, 4, 5)
         lev_mm(3, 4, None)
-        f_mm(6); f_out(6); f_mm(7); f_out(7)
-        dma("sy", T.fp[:, 4 * C:8 * C], T.fp[:, 0:4 * C], ["fp.%d" % b for b in range(4)], ["fp2"], "fpd")
         level(2, 1, 2)
         if r == 0:
             ts(T.mask16[:], T.j16[:], col("q"), -1.0, OP.is_equal, OP.mult, ["j16", "c.q"], ["mask16"])
@@ -428,11 +452,8 @@ def rank_program(g, core, T, topo):
             tt(T.ex[:, c], T.t[:, c], T.mask16[:, c], OP.mult, Tk + ["mask16"], ["ex.%d" % h])
             scan(T.scx[:, c], T.r16[:, c], T.ex[:, c], 0.0, OP.mult, OP.add, ["r16", "ex.%d" % h], ["scx.%d" % h])
         for a in range(NA):
-            emit("a", lambda a=a: s_.activation(T.junk[:, C * a:C * a + C], T.t[:], ActivationFunctionType.Sign, bias=T.scx[:, 16 * a + 15:16 * a + 16],
+            emit("a", lambda a=a: s_.activation(T.junk[:, C * a:C * a + C], T.t[:], AF.Sign, bias=T.scx[:, 16 * a + 15:16 * a + 16],
                                                 accum_out=T.acc[:, a:a + 1]), Tk + ["scx.%d" % (a // 9)], ["acc.%d" % a])
-        if r == 0:
-            fill(T.r144[:], 1.0, "r144")
-            fill(T.r144[:, 0:C:144], 0.0, "r144")
 
         def cmp_scan(j):
             scan(T.cs[:, C * j:C * j + C], T.r144[:], T.cf[:, C * j:C * j + C], 0.0, OP.mult, OP.add, ["r144", "cf.%d" % j], ["cs.%d" % j])
@@ -441,7 +462,7 @@ def rank_program(g, core, T, topo):
             ts(T.cf[:, C * j:C * j + C], T.t[:], T.scx[:, 16 * a + 15:16 * a + 16], 0.0, OP.add, OP.is_lt, Tk + ["scx.1"], ["cf.%d" % j])
             if j > 0:
                 cmp_scan(j - 1)
-        x1, y1, lo, z, e1, e2, en = [T.sm[:, i:i + 1] for i in range(7)]
+        x1, y1, lo, z, e1, e2 = [T.sm[:, i:i + 1] for i in range(6)]
         tt(lo, x1, y1, OP.subtract, ["x1", "y1"], ["lo"])
         cmp_scan(NV - 1)
         ts(z, lo, magic(64), magic(64), OP.add, OP.subtract, ["lo"], ["z"])
@@ -453,8 +474,6 @@ def rank_program(g, core, T, topo):
         emit("v", lambda: v.transpose(T.trb[:], T.bcb[:]), ["bcb"], ["trb"])
         tt(T.val[:], T.trb[:, 0:32].indirect(T.list3[:, 0:18]), T.own[:], OP.add, ["trb", "own", "list3.0", "list3.1"], ["val"])
         if r == 0:
-            floor_to("k4", "q", 4)
-            cs("e", "k4", -1.0, col("q"), OP.mult, OP.add, "q")
             cs("eo", "e", 576.0, None, OP.add, None)
             ts(T.mask4[:], T.j4[:], col("k4"), None, OP.is_equal, None, ["j4", "c.k4"], ["mask4"])
         ts(T.off[:, 0:NA], T.acc[:], -0.5, 143.5, OP.mult, OP.add, ["acc.%d" % a for a in range(NA)], ["off.a"])
@@ -465,7 +484,6 @@ def rank_program(g, core, T, topo):
         ts(T.ta[:, 0:32], W, magic(512), magic(512), OP.add, OP.subtract, ["sc.0"], ["ta"])
         tt(T.oa[:, 0:32], W, T.ta[:, 0:32], OP.subtract, ["sc.0", "ta"], ["oa"])
         ts(T.lu[:], T.oa[:, 0:32], 4.0, col("eo"), OP.mult, OP.add, ["oa", "c.eo"], ["lu"])
-        fhk = ["fh.%d" % b for b in range(4)]
         for h in range(2):
             act(T.g1[:, 256 * h:256 * h + 256], T.fh[:, 0:4 * C].indirect(T.lu[:, 16 * h:16 * h + 16]), fhk + ["lu"], ["g1.%d" % h])
         ts(T.la[:], T.oa[:, 0:32], 4.0, col("eo"), OP.mult, OP.add, ["oa", "c.eo"], ["la"])
@@ -474,32 +492,25 @@ def rank_program(g, core, T, topo):
         emit("v", lambda: v.tensor_copy(T.bu[:], T.lb[:]), ["lb"], ["bu"])
         for h in range(2):
             tt(T.zt[:, 256 * h:256 * h + 256], T.fp[:, 0:8 * C].indirect(T.bu[:, 16 * h:16 * h + 16]), T.g1[:, 256 * h:256 * h + 256], OP.add,
-               ["fp.%d" % b for b in range(4)] + ["fp2", "bu", "g1.%d" % h], ["zt.%d" % h])
+               fpk + ["bu", "g1.%d" % h], ["zt.%d" % h])
         quant("z", K * r, K * r + K, T.zt[:], ["zt.0", "zt.1"], ["qz%d" % r])
 
         def send():
-            tr = []
-            sem = T.sem[("arr%d" if direct else "rar%d") % r]
-            for j in range(4):
-                d = nxt if direct else hopmates[j]
-                es = topo.engines(core, d)
-                rid, pid = topo.addr(d, core)
-                dst = T.qa[:, K * r + 32 * j:K * r + 32 * j + 32] if direct else T.rq[:, 32 * r:32 * r + 32]
-                tr.append(RemoteDMATransfer(dst_ids=[DstId(rid=rid, pnc=pid)], dma_engine_mask=bits(es[2 * j:2 * j + 2]),
-                                            remote_sem=sem, src=u8(T.qz[:, K * r + 32 * j:K * r + 32 * j + 32]), dst=u8(dst)))
-            d = nxt if direct else hopmates[0]
-            es = topo.engines(core, d)
-            rid, pid = topo.addr(d, core)
-            tr.append(RemoteDMATransfer(dst_ids=[DstId(rid=rid, pnc=pid)], dma_engine_mask=bits(es[len(es) // 2:]),
-                                        remote_sem=sem, src=T.sz[:, K * r:K * r + K], dst=(T.sa if direct else T.rs)[:, K * r:K * r + K]))
-            g.remote_dma_fused(tr, local_sem=T.sem.snt)
-            return 8 + len(es) // 2
-        cnt = [0]
-
-        def do_send():
-            cnt[0] = send()
-        emit("g", do_send, ["qz%d" % r], [])
-        sent += cnt[0]
+            z = slice(K * r, K * r + K)
+            if direct:
+                es, sem = topo.engines(core, nxt)[:8], T.sem["arr%d" % r]
+                g.remote_dma_fused([move(topo, core, nxt, es, sem, u8(T.qa[:, z]), u8(T.qz[:, z]))], local_sem=T.sem.snt)
+                g.remote_dma_fused([move(topo, core, nxt, es, sem, T.sa[:, z], T.sz[:, z])], local_sem=T.sem.snt)
+                sent.append(2 * len(es))
+                return
+            sem = T.sem["rar%d" % r]
+            es = topo.engines(core, hopmates[0])
+            m = len(es) // 2
+            g.remote_dma_fused([move(topo, core, hopmates[j], es[m * j:m * j + m], sem, u8(T.rq[:, 64 * r:64 * r + 64]),
+                                     u8(T.qz[:, K * r + 64 * j:K * r + 64 * j + 64])) for j in range(2)], local_sem=T.sem.snt)
+            g.remote_dma_fused([move(topo, core, hopmates[2], es, sem, T.rs[:, z], T.sz[:, z])], local_sem=T.sem.snt)
+            sent.append(2 * len(es))
+        emit("g", send, ["qz%d" % r], [])
 
         tt(T.ml[:, K:C], T.lin[:, K:C], T.mask4[:, K:C], OP.mult, ["lin", "mask4"], ["ml.1"])
         scan(T.sc[:, K:C], T.r4[:, K:C], T.ml[:, K:C], 0.0, OP.mult, OP.add, ["r4", "ml.1"], ["sc.1"])
@@ -507,17 +518,21 @@ def rank_program(g, core, T, topo):
         ts(T.tsv[:], W2, magic(512), magic(512), OP.add, OP.subtract, ["sc.1"], ["tsv"])
         tt(T.osv[:], W2, T.tsv[:], OP.subtract, ["sc.1", "tsv"], ["osv"])
         ts(T.sul[:], T.osv[:], 4.0, col("eo"), OP.mult, OP.add, ["osv", "c.eo"], ["sul"])
-        act(T.xs[:], T.fh[:, 0:4 * C].indirect(T.sul[:, 0:40]), fhk + ["sul"], ["xs"], scale=2.0)
-        if r == R - 1:
-            ts(T.o1[:], T.lin[:], magic(512), magic(512), OP.add, OP.subtract, ["lin"], ["o1"])
-            tt(T.o2[:], T.lin[:], T.o1[:], OP.subtract, ["lin", "o1"], ["o2"])
-        quant("x", 0, NS, T.xs[:], ["xs"], ["qxs"])
+        act(T.xs[:, 0:320], T.fh[:, 0:4 * C].indirect(T.sul[:, 0:20]), fhk + ["sul"], ["xs"], scale=2.0)
+        ts(T.xs[:, 320:640], T.fh[:, 0:4 * C].indirect(T.sul[:, 20:40]), 2.0, None, OP.mult, None, fhk + ["sul"], ["xs.v"])
+        quant("x", 0, NS, T.xs[:], ["xs", "xs.v"], ["qxs"])
         if r < R - 1:
             front(0)
             for l in (1, 2, 3):
                 list_mm(l, 0, l)
             for l in (1, 2, 3):
                 list_out(l, 0, l)
+            mm(4, NS, "m0", 0, "f", 10, ["qm0", "qfs"])
+            mm(5, NS, "p0", 0, "f", 10, ["qp0", "qfs"])
+            for k in range(8):
+                scan(T.t[:, k:NS:8], T.zf[:, k:NS:8], T.ps4[:, k:NS:8], -1.0e6, OP.max, OP.add, ["zf", "ps4"], [Tk[k], "th.%d" % k])
+            tt(T.pv[:, 0:NS], T.t[:, 0:NS], T.ps5[:, 0:NS], OP.add, Tk + ["ps5"], ["pvs"])
+            emit("v", lambda: v.tensor_reduce(T.sm[:, 8:9], T.pv[:, 0:NS], AxisListType.X, OP.min), ["pvs"], ["xs1"])
         else:
             ts(T.jn[:], T.jn[:], col("q"), None, OP.add, None, ["jn", "c.q"], ["jn"])
             ts(T.jk[:], T.jn[:], 1.0 / 36.0, -17.5 / 36.0, OP.mult, OP.add, ["jn"], ["jk"])
@@ -527,19 +542,23 @@ def rank_program(g, core, T, topo):
             tt(T.jn[:], T.jn[:], T.jk[:], OP.add, ["jn", "jk"], ["jn"])
             emit("v", lambda: v.tensor_copy(T.nat[:], T.jn[:]), ["jn"], ["nat"])
             quant("v", 0, 128, T.vt[:], ["vt"], ["qv"])
+            ts(T.o1[:], T.lin[:], magic(512), magic(512), OP.add, OP.subtract, ["lin"], ["o1"])
+            tt(T.o2[:], T.lin[:], T.o1[:], OP.subtract, ["lin", "o1"], ["o2"])
             ts(T.o3[:], T.o2[:], 140.5, magic(8), OP.add, OP.add, ["o2"], ["o3"])
             ts(T.o1[:], T.o2[:], 36.0, 5184.0, OP.mult, OP.add, ["o2"], ["o1"])
             ts(T.o4[:], T.o3[:], magic(8), -35.875, OP.subtract, OP.mult, ["o3"], ["o4"])
             tt(T.opt[:], T.o1[:], T.o4[:], OP.add, ["o1", "o4"], ["opt"])
             dma("sy", T.op[:], T.opt[0:128:16, :], ["opt"], [], "od")
 
-        ne = 4 * 4 + 4 if indirect_in else 8 + len(topo.engines(prv, core)) // 2
+        ne = 3 * len(topo.engines(indirect_in[0], core)) if indirect_in else 16
         g.tensor.wait_ge(T.sem["arr%d" % r], ne)
         for b in range(4):
-            mm(b, K, "w", 128 * b, "a", K * r, ["qw", "sw"])
-            act(T.tm[:, K * b:K * b + K], T["ps%d" % b][:, 0:K], ["ps%d" % b], ["tm.%d" % b], scale=0.0078125)
-            mm(4 + b, K, "e%d" % b, 0, "a", K * r, ["qe%d" % b])
-            tt(T.xh[:, b:512:4], T.tm[:, K * b:K * b + K], T["ps%d" % (4 + b)][:, 0:K], OP.add, ["tm.%d" % b, "ps%d" % (4 + b)], ["xh.%d" % b])
+            mm(b, K, "w", 128 * b, "a", K * r, ["qw", "sw"], stop=False)
+            mm(b, K, "e%d" % b, 0, "a", K * r, ["qe%d" % b], start=False)
+            if b % 2 == 0:
+                act(T.xh[:, b:512:4], T["ps%d" % b][:, 0:K], ["ps%d" % b], ["xh.%d" % b], scale=0.0078125)
+            else:
+                ts(T.xh[:, b:512:4], T["ps%d" % b][:, 0:K], 0.0078125, None, OP.mult, None, ["ps%d" % b], ["xh.%d" % b])
         quant("x", NS, C, T.xh[:], ["xh.%d" % b for b in range(4)], ["qxh"])
 
     emit("v", lambda: v.tensor_copy(T.qn[:, 0:C].bitcast(dt.uint32), T.qx[:, 0:C].bitcast(dt.uint32).indirect(T.nat[:, 0:18])), qx + ["nat"], ["qn"])
@@ -552,4 +571,4 @@ def rank_program(g, core, T, topo):
     dma("sy", T.y[:], T.yt[:], ["yt"], [], "od")
     for s in count:
         g.wait_ge(T.sem[s], count[s])
-    g.wait_ge(T.sem.snt, sent)
+    g.wait_ge(T.sem.snt, sum(sent))

from concourse.bass import DstId, RemoteDMATransfer
from concourse.mybir import dt, AluOpType, AxisListType, ActivationFunctionType

OP = AluOpType
AF = ActivationFunctionType
CP = AF.Copy
C, K, R, NS, NH = 288, 128, 3, 160, 128
SOURCE = [7, 0, 1, 1, 2, 2, 3, 3]
NA = 13
NV = 18 - NA
THR = 1572864.0
BIG = 2097152.0


def magic(step):
    return float(1.5 * 2.0 ** 23 * step)


SCRATCH = {}


def buf(name, n, dtype="float32", where="sbuf"):
    SCRATCH[name] = (where, [128, n], dtype)


CODE = "float8_e4m3fn_x4"


def pair(name, n):
    buf("q" + name, n, CODE)
    buf("s" + name, n, "uint8")


for _b in range(8):
    buf("ps%d" % _b, 512, "float32", "psum")
buf("xt", 4 * C, "bfloat16"); buf("ut", 512, "bfloat16"); buf("vt", 512, "bfloat16")
pair("u0", 128); pair("u", 128); pair("v", 128); pair("w", 512); pair("x", C); pair("n", C); pair("f", 306)
CONST = {n: 128 * i for i, n in enumerate(["m0", "m1", "m2", "m3", "p0", "p1", "p2", "k1", "k2", "k3", "e0", "e1", "e2", "e3"])}
pair("k", 128 * len(CONST))
for _l in (1, 2, 3):
    buf("kt%d" % _l, 512, "bfloat16")
    buf("list%d" % _l, 18, "uint16")
    buf("thr%d" % _l, 32)
pair("z", R * K); pair("a", R * K)
buf("rq", 64 * R, CODE); buf("rs", K * R, "uint8")
buf("pc", 64); buf("pi", 8, "int32"); buf("ab", 128); buf("st", 512, "bfloat16"); buf("zero", 680, "bfloat16")
buf("gm0", 128); buf("gm1", 128); buf("gm2", 128); buf("gm3", 128)
buf("m8", 128, "int32"); buf("mb", 128, "int32"); buf("mc", 128, "int32"); buf("xp", 128); buf("eq", 128)
buf("i3", 128)
for _t in range(4):
    buf("ct%d" % _t, 128)
buf("one", 128, "bfloat16"); buf("idt", 520, "bfloat16")
buf("onef", C); buf("j16", C); buf("j4", C); buf("mask16", C); buf("mask4", C); buf("r16", C); buf("r4", C)
buf("r144", C, "bfloat16")
buf("zf", C); buf("d0a", C); buf("d0b", C); buf("own", C); buf("z32", 32)
buf("jn", 18); buf("jk", 18); buf("nat", 18, "uint16")
buf("ja", 8); buf("jb", 8); buf("ul", 8, "uint16")
buf("fls", 680, "bfloat16"); buf("flh", 544, "bfloat16")
buf("t", C); buf("wt", C); buf("pv", C); buf("sm", 16); buf("bc", 32); buf("tr", 32); buf("bcb", 32); buf("trb", 32)
buf("val", C); buf("ex", C); buf("scx", C); buf("cf", NV * C, "bfloat16"); buf("cs", NV * C, "bfloat16")
buf("junk", NA * C, "bfloat16"); buf("acc", NA); buf("rkv", NV); buf("off", 18, "uint16")
buf("lin", C); buf("ml", C); buf("sc", C)
buf("ta", 40); buf("oa", 40); buf("la", 32); buf("lb", 32); buf("lu", 32, "uint16"); buf("bu", 32, "uint16")
buf("tsv", 40); buf("osv", 40); buf("sul", 40, "uint16")
buf("fh", 4 * C, "bfloat16"); buf("fp", 8 * C, "bfloat16")
buf("g1", 512); buf("zt", 512, "bfloat16"); buf("xs", 640, "bfloat16"); buf("xh", 512, "bfloat16")
buf("o1", C); buf("o2", C); buf("o3", C); buf("o4", C); buf("opt", C); buf("yt", C)

SEMAPHORES = ["ev", "ea", "ep", "eg", "lx", "lu", "lw", "lws", "lv", "fpd", "od", "snt"]
SEMAPHORES += ["arr%d" % _r for _r in range(R)] + ["rar%d" % _r for _r in range(R)]


def relays(topo, a, b):
    if topo.may_write(a, b):
        return []
    own = [c for c in topo.cores_of(a) if c != a and topo.may_write(c, b)]
    other = [c for c in own if topo.die(c) != topo.die(own[0])]
    return [own[0], other[0], [c for c in own if c not in (own[0], other[0])][0]]


def bits(es):
    return sum(1 << e for e in es)


def u8(ap):
    return ap.bitcast(dt.uint8)


def move(topo, src, dst, es, sem, out, in_):
    rid, pid = topo.addr(dst, src)
    return RemoteDMATransfer(dst_ids=[DstId(rid=rid, pnc=pid)], dma_engine_mask=bits(es), remote_sem=sem, src=in_, dst=out)


def relay_program(g, core, T, topo):
    for i, a in enumerate(T.cores):
        b = T.cores[(i + 1) % len(T.cores)]
        rl = relays(topo, a, b)
        if core not in rl:
            continue
        j = rl.index(core)
        es = topo.engines(core, b)
        for r in range(R):
            if j < 2:
                n, o = len(topo.engines(a, core)) // 2, K * r + 64 * j
                out, in_ = u8(T.qa[:, o:o + 64]), u8(T.rq[:, 64 * r:64 * r + 64])
            else:
                n, out, in_ = len(topo.engines(a, core)), T.sa[:, K * r:K * r + K], T.rs[:, K * r:K * r + K]
            g.wait_ge(T.sem["rar%d" % r], n)
            g.remote_dma_fused([move(topo, core, b, es, T.sem["arr%d" % r], out, in_)], local_sem=T.sem.snt)
        g.wait_ge(T.sem.snt, R * len(es))


def rank_program(g, core, T, topo):
    rank = T.rank_of(core)
    if rank is None:
        relay_program(g, core, T, topo)
        return
    N = len(T.cores)
    nxt, prv = T.cores[(rank + 1) % N], T.cores[(rank - 1) % N]
    queue = {"v": g.vector, "a": g.scalar, "p": g.tensor, "g": g, "sy": g.sync}
    count = {}
    known = {q: {} for q in queue}
    wr, rd = {}, {}

    def emit(q, fn, reads, writes, sem=None, inc=1, acc=False):
        sem = sem or "e" + q
        need = {}

        def dep(d):
            need[d[1]] = max(need.get(d[1], 0), d[2])
        for k in reads:
            for d in wr.get(k, []):
                dep(d)
            if k.startswith("ps"):
                for d in rd.get(k, []):
                    if d[0] != q:
                        dep(d)
        for k in writes:
            for d in wr.get(k, []) + rd.get(k, []):
                if not (acc and d[0] == q):
                    dep(d)
        for s in need:
            if known[q].get(s, 0) < need[s]:
                queue[q].wait_ge(T.sem[s], need[s])
                known[q][s] = need[s]
        ins = fn()
        if ins is None:
            return
        ins.then_inc(T.sem[sem], inc)
        count[sem] = count.get(sem, 0) + inc
        d = (q, sem, count[sem])
        for k in writes:
            wr[k] = [d]
            rd[k] = []
        for k in reads:
            rd[k] = [e for e in rd.get(k, []) if e[1] != sem] + [d]

    v, s_, te = g.vector, g.scalar, g.tensor

    def ts(out, in0, s1, s2, op0, op1, reads, writes):
        if op1 is None:
            emit("v", lambda: v.tensor_scalar(out, in0, s1, None, op0), reads, writes)
        else:
            emit("v", lambda: v.tensor_scalar(out, in0, s1, s2, op0, op1), reads, writes)

    def tt(out, in0, in1, op, reads, writes):
        emit("v", lambda: v.tensor_tensor(out, in0, in1, op), reads, writes)

    def scan(out, d0, d1, init, op0, op1, reads, writes):
        emit("v", lambda: v.tensor_tensor_scan(out, d0, d1, init, op0, op1), reads, writes)

    def quant(name, a, b, tile, reads, writes):
        if name in CONST:
            a, b, name = CONST[name] + a, CONST[name] + b, "k"
        emit("v", lambda: v.quantize_mx(T["q" + name][:, a:b], T["s" + name][:, a:b], tile), reads, writes)

    def act(out, in_, reads, writes, scale=1.0):
        emit("a", lambda: s_.activation(out, in_, CP, scale=scale), reads, writes)

    def mm(bank, n, st, so, mv, a, reads, start=True, stop=True):
        if st in CONST:
            so, st = CONST[st], "k"
        emit("p", lambda: te.matmul_mx(T["ps%d" % bank][:, 0:n], T["q" + st][:, so:so + 128], T["s" + st][:, so:so + 128],
                                       T["q" + mv][:, a:a + n], T["s" + mv][:, a:a + n], start, stop), reads, ["ps%d" % bank], acc=not start)

    def fill(ap, c, w):
        emit("v", lambda: v.memset(ap, c), [], [w])

    def iota(ap, pat, base, cm, w, ints=False):
        if ints:
            emit("g", lambda: g.iota(ap, pat, base, cm), [], [w])
        else:
            emit("g", lambda: g.iota(ap, pat, base, cm, allow_small_or_imprecise_dtypes=True), [], [w])

    def aff(out, in_, pat, op, fillv, base, cm, reads, writes):
        emit("g", lambda: g.affine_select(out, in_, pat, op, fillv, base, cm), reads, writes)

    def dma(q, out, in_, reads, writes, sem, acc=False):
        emit(q, lambda: queue[q].dma_start(out, in_), reads, writes, sem, 16, acc)

    dma("sy", T.xt[:], T.x[:], [], ["xt"], "lx")
    dma("a", T.ut[:], T.u[:], [], ["ut"], "lu")
    dma("sy", u8(T.qw[:]), T.wc[:], [], ["qw"], "lw")
    dma("sy", T.sw[:], T.ws[:], [], ["sw"], "lws")
    dma("sy", T.vt[:], T.v[:], [], ["vt"], "lv")

    names = []

    def col(n):
        if n not in names:
            names.append(n)
        i = names.index(n)
        return T.pc[:, i:i + 1]

    def cs(out, in0, s1, s2, op0, op1, *reads):
        ts(col(out), col(in0), s1, s2, op0, op1, ["c." + x for x in (in0,) + reads], ["c." + out])

    iota(T.pi[:, 0:1], [[0, 1]], 0, 1, "pi", True)
    iota(col("p"), [[0, 1]], 0, 1, "c.p")
    iota(T.ja[:], [[0, 4], [16, 2]], 0, 0, "ja")
    iota(T.gm0[:], [[1, 1], [0, 128]], 0, 0, "gm0")
    iota(T.m8[:], [[0, 16], [1, 8]], 0, 0, "m8", True)
    iota(T.i3[:], [[4, 8], [0, 4], [1, 4]], 0, 0, "i3")
    for t in range(4):
        aff(T["ct%d" % t][:], T.i3[:], [[0, 8], [1, 4], [0, 4]], OP.is_equal, -1.0, -t, 0, ["i3"], ["ct%d" % t])
    for l in range(1, 4):
        iota(T["gm%d" % l][:], [[1, 2 ** l], [0, 128 >> l]], 0, 0, "gm%d" % l)
    fill(T.st[:], 0.0, "st")
    fill(T.zero[:], 0.0, "zero")
    for n, w in (("fls", 680), ("flh", 544), ("idt", 520)):
        act(T[n][:], T.zero[:, 0:w], ["zero"], [n])
    iota(T.zf[:], [[0, C]], 0, 0, "zf")
    iota(T.z32[:], [[0, 32]], int(THR), 0, "z32")
    for l in (1, 2, 3):
        aff(T["thr%d" % l][:], T.z32[:], [[0, 32]], OP.is_ge, 0.0, -(128 >> l), 1, ["z32"], ["thr%d" % l])
    iota(T.one[:], [[0, 128]], 128, 0, "one")
    aff(T.idt[:, 4:516:4], T.one[:], [[-1, 128]], OP.is_equal, 0.0, 0, 1, ["one", "idt"], ["idt"])
    iota(T.d0a[:], [[64, 8], [1, 36]], -274, 0, "d0a")
    iota(T.j16[:], [[0, 18], [1, 16]], 0, 0, "j16")
    iota(T.onef[:], [[0, C]], 1, 0, "onef")
    aff(T.r16[:], T.onef[:], [[0, 18], [1, 16]], OP.not_equal, 0.0, 0, 0, ["onef"], ["r16"])
    iota(T.r144[:], [[0, C]], 1, 0, "r144")
    aff(T.r144[:], T.r144[:], [[0, 2], [1, 144]], OP.not_equal, 0.0, 0, 0, ["r144"], ["r144"])
    iota(T.own[:], [[1, C]], -144, 0, "own")
    iota(T.j4[:], [[0, 72], [4, 4]], 0, 0, "j4")
    aff(T.r4[:], T.onef[:], [[0, 72], [1, 4]], OP.not_equal, 0.0, 0, 0, ["onef"], ["r4"])
    iota(T.jn[:], [[16, 18]], 0, 0, "jn")
    iota(T.d0b[:], [[1, 36], [64, 8]], -274, 0, "d0b")

    low = [("r", 31), ("q", 15), ("q32", 96), ("odd", 16), ("k4", 12), ("e", 3), ("qb", 32)]
    for n, m in low:
        col(n)
    for j, (n, m) in enumerate(low):
        ts(T.pi[:, j + 1:j + 2], T.pi[:, 0:1], m, None, OP.bitwise_and, None, ["pi"], ["pi.%d" % j])
    emit("v", lambda: v.tensor_copy(T.pc[:, 1:8], T.pi[:, 1:8]), ["pi.%d" % j for j in range(7)], ["c." + n for n, m in low])
    cs("g3", "r", 1.0 / 3.0, -1.0 / 3.0, OP.mult, OP.add)
    ts(T.ja[:], T.ja[:], col("q"), None, OP.add, None, ["ja", "c.q"], ["ja"])
    cs("G", "g3", magic(1), magic(1), OP.add, OP.subtract)
    ts(T.jb[:], T.ja[:], 1.0 / 3.0, -1.0 / 3.0, OP.mult, OP.add, ["ja"], ["jb"])
    cs("i", "G", -3.0, col("r"), OP.mult, OP.add, "r")
    ts(T.jb[:], T.jb[:], magic(1), magic(1), OP.add, OP.subtract, ["jb"], ["jb"])
    cs("i0", "i", 0.0, None, OP.is_equal, None)
    ts(T.jb[:], T.jb[:], 13.0, None, OP.mult, None, ["jb"], ["jb"])
    cs("wk0", "i0", 1.0, col("i"), OP.mult, OP.subtract, "i")
    tt(T.jb[:], T.jb[:], T.ja[:], OP.add, ["jb", "ja"], ["jb"])
    cs("wk", "wk0", 3.0, None, OP.add, None)
    ts(T.ul[:], T.jb[:], 127.0, None, OP.min, None, ["jb"], ["ul"])
    cs("v", "qb", 0.0, None, OP.is_equal, None)
    cs("a1", "p", 32.0, col("wk"), OP.is_lt, OP.mult, "wk")
    cs("a2", "p", 64.0, col("i0"), OP.is_lt, OP.mult, "i0")
    cs("a3", "p", 64.0, col("i0"), OP.is_ge, OP.mult, "i0")
    cs("a4", "a1", 1.0, col("a2"), OP.mult, OP.add, "a2")
    cs("wM0", "a4", 1024.0, None, OP.mult, None)
    cs("wM1", "a4", 1024.0, col("a3"), OP.mult, OP.add, "a3")

    def hit(out, in_, c, w, reads, writes):
        emit("a", lambda: s_.activation(T.ab[:], in_, AF.Abs, bias=col(c), scale=-1.0), reads + ["c." + c], ["ab"])
        emit("a", lambda: s_.activation(out, T.ab[:], AF.Relu, bias=col(w), scale=col("n" + w)), ["ab", "c." + w, "c.n" + w], writes)

    for w in ("wM0", "wM1", "wk"):
        cs("n" + w, w, -1.0, None, OP.mult, None)

    def const_m(l):
        w = "wM%d" % (l // 2)
        hit(T.st[:, 0:512:4], T["gm%d" % l][:], "G", w, ["gm%d" % l, "st"], ["st"])
        quant("m%d" % l, 0, 128, T.st[:], ["st"], ["qm%d" % l])

    def const_p(l):
        ts(T.eq[:], T["gm%d" % l][:], col("G"), None, OP.is_equal, None, ["gm%d" % l, "c.G"], ["eq"])
        tt(T.st[:, 0:512:4], T.eq[:], T.xp[:], OP.mult, ["eq", "xp", "st"], ["st"])
        quant("p%d" % l, 0, 128, T.st[:], ["st"], ["qp%d" % l])

    quant("u0", 0, 128, T.ut[:], ["ut"], ["qu0"])
    emit("v", lambda: v.tensor_copy(T.qu[:, 0:128].bitcast(dt.uint32), T.qu0[:, 0:128].bitcast(dt.uint32).indirect(T.ul[:, 0:8])), ["qu0", "ul"], ["qu"])
    emit("a", lambda: s_.activation(T.su[:, 0:128], T.su0[:, 0:128].indirect(T.ul[:, 0:8]), CP), ["qu0", "ul"], ["su"])
    quant("x", 0, NS, T.xt[:, 0:4 * NS], ["xt"], ["qxs"])
    quant("x", NS, C, T.xt[:, 4 * NS:4 * C], ["xt"], ["qxh"])
    const_m(0)
    cs("G4", "G", 4.0, None, OP.mult, None)
    cs("pw0", "i", 2.0, col("i"), OP.is_equal, OP.add, "i")
    cs("R", "q32", 1.0 / 32.0, col("G4"), OP.mult, OP.add, "G4")
    cs("pw", "pw0", 1.0, None, OP.add, None)
    cs("v4", "v", 4.0, None, OP.mult, None)
    cs("wP", "p", 64.0, BIG, OP.is_lt, OP.mult)
    for t in range(4):
        hit(T.kt3[:, t:512:4], T["ct%d" % t][:], "R", "wk", ["ct%d" % t], ["kt3.%d" % t])
    k3 = ["kt3.%d" % t for t in range(4)]
    for gg in range(8):
        a = 64 * (gg // 2)
        act(T.kt2[:, 64 * gg:64 * gg + 64], T.kt3[:, a:a + 64], k3, ["kt2.%d" % gg])
    for h in range(4):
        a = 128 * (h // 2)
        act(T.kt1[:, 128 * h:128 * h + 128], T.kt2[:, a:a + 128], ["kt2.%d" % x for x in range(4)], ["kt1.%d" % h])

    MAPS = [dict(d0="d0a", sl=lambda k: (36 * k, 36 * k + 36, 1), al=1.0, be=0.4375, ga=161.0),
            dict(d0="d0b", sl=lambda k: (k, C, 8), al=8.0, be=7.984375, ga=140.0)]

    def front(h):
        f, n, o, w, b = ("flh", NH, 0, 512, 0) if h else ("fls", NS, 40, 0, 0)
        S = T["ps%d" % b]
        mm(b, n, "u", 0, "x", NS if h else 0, ["qu", "su", "qxh" if h else "qxs"])
        F = T[f]
        ts(F[:, o:o + 4 * n:4], S[:, 0:n], 0.0, col("v"), OP.is_gt, OP.is_equal, ["ps%d" % b, "c.v"], [f])
        for Q in range(4):
            ts(F[32 * Q:32 * Q + 32, w:w + n // 4], S[32 * Q:32 * Q + 32, Q:n:4], 0.0, None, OP.is_gt, None, ["ps%d" % b], [f + ".%d" % Q])
        rds = [f] + [f + ".%d" % Q for Q in range(4)]
        if h:
            quant("f", 170, 306, F[:, 0:544], rds, ["qfh"])
        else:
            quant("f", 0, 170, F[:, 0:680], rds, ["qfs"])

    def list_mm(l, h, bank):
        if h:
            mm(bank, 128, "k%d" % l, 0, "f", 178, ["qk%d" % l, "qfh"])
        else:
            mm(bank, 128, "k%d" % l, 0, "f", 0, ["qk%d" % l, "qfs"])

    def list_out(l, h, bank):
        a, b, i = (10, 18, 120) if h else (0, 10, 0)
        ts(T["list%d" % l][:, a:b], T["ps%d" % bank][:, i:i + b - a], col("odd"), None, OP.add, None, ["ps%d" % bank, "c.odd"], ["list%d.%d" % (l, h)])

    front(0)
    ts(T.mb[:], T.m8[:], col("pw"), None, OP.mult, None, ["m8", "c.pw"], ["mb"])
    ts(T.mc[:], T.mb[:], 4, None, OP.bitwise_and, None, ["mb"], ["mc"])
    ts(T.xp[:], T.mc[:], col("v4"), col("wP"), OP.not_equal, OP.mult, ["mc", "c.v4", "c.wP"], ["xp"])
    const_p(0)
    for l in (3, 2, 1):
        quant("k%d" % l, 0, 128, T["kt%d" % l][:], k3 if l == 3 else ["kt2.%d" % x for x in range(8)] if l == 2 else ["kt1.%d" % x for x in range(4)], ["qk%d" % l])

    qx = ["qxs", "qxh"]
    qf = ["qfs", "qfh"]
    Tk = ["t.%d" % k for k in range(8)]
    direct = topo.may_write(core, nxt)
    hopmates = relays(topo, core, nxt)
    indirect_in = relays(topo, prv, core)
    fhk = ["fh.%d" % b for b in range(4)]
    fpk = ["fp.%d" % x for x in range(16)]
    sent = []

    for r in range(R):
        mp = MAPS[0 if r == 0 else 1]
        D0 = T[mp["d0"]]
        view = lambda buf_, k: buf_[:, mp["sl"](k)[0]:mp["sl"](k)[1]:mp["sl"](k)[2]]
        front(1)
        if r == 0:
            for l in (1, 2, 3):
                list_mm(l, 0, l)
            for l in (1, 2, 3):
                list_out(l, 0, l)

        def unpack(j):
            mm(6 + j % 2, C, "e%d" % j, 0, "x", 0, ["qe%d" % j] + qx)
            act(T.fh[:, j:4 * C:4], T["ps%d" % (6 + j % 2)][:, 0:C], ["ps%d" % (6 + j % 2)], ["fh.%d" % j], scale=0.5 / 128)

        def lev_mm(l, bank, pb):
            mm(bank, C, "m%d" % l, 0, "f", 10, ["qm%d" % l] + qf)
            if pb is not None:
                mm(pb, C, "p%d" % l, 0, "f", 10, ["qp%d" % l] + qf)

        if r == 0:
            lev_mm(0, 1, 2)
            const_m(1)
            const_p(1)
        else:
            unpack(0)
            unpack(1)
            mm(1, NH, "m0", 0, "f", 170, ["qm0", "qfh"])
            mm(2, NH, "p0", 0, "f", 170, ["qp0", "qfh"])
        list_mm(1, 1, 3)
        lev_mm(1, 4, 5)
        list_mm(2, 1, 0)

        def level(l, bank, pb):
            x1, y1, xs, xh = T.sm[:, 0:1], T.sm[:, 1:2], T.sm[:, 8:9], T.sm[:, 9:10]
            B, P = T["ps%d" % bank], T["ps%d" % pb] if l < 3 else None
            if l == 0 and r > 0:
                for k in range(8):
                    scan(T.t[:, NS + k:C:8], T.zf[:, NS + k:C:8], B[:, k:NH:8], T.t[:, NS - 8 + k:NS - 7 + k], OP.max, OP.add, ["zf", "ps%d" % bank, Tk[k]], ["th.%d" % k])
                tt(T.pv[:, NS:C], T.t[:, NS:C], P[:, 0:NH], OP.add, ["th.%d" % k for k in range(8)] + ["ps%d" % pb], ["pv"])
                emit("v", lambda: v.tensor_reduce(xh, T.pv[:, NS:C], AxisListType.X, OP.min), ["pv"], ["xh1"])
                list_out(1, 1, 3)
                tt(x1, xh, xs, OP.min, ["xh1", "xs1"], ["x1"])
            else:
                d0, dk = (T.zf, "zf") if l == 0 else (T.wt, "wt")
                for k in range(8):
                    scan(view(T.t, k), view(d0, k), view(B, k), -1.0e6, OP.max, OP.add, [dk, "ps%d" % bank], [Tk[k], "th.%d" % k])
                if l == 3:
                    return
                tt(T.pv[:], T.t[:], P[:, 0:C], OP.add, Tk + ["ps%d" % pb], ["pv", "pvs"])
                emit("v", lambda: v.tensor_reduce(x1, T.pv[:], AxisListType.X, OP.min), ["pv"], ["x1"])
                list_out(l + 1, 1, {1: 3, 2: 0, 3: 3}[l + 1])
            th, w = "thr%d" % (l + 1), x1
            if l == 2:
                ts(y1, x1, magic(1024), magic(1024), OP.add, OP.subtract, ["x1"], ["y1"])
                w = y1
            ts(T.bc[:], T[th][:], x1, w, OP.is_gt, OP.mult, [th, "x1", "y1"], ["bc"])
            emit("v", lambda: v.transpose(T.tr[:], T.bc[:]), ["bc"], ["tr"])
            win = T.tr[:, 0:32].indirect(T["list%d" % (l + 1)][:, 0:18])
            ll = ["tr", "list%d.0" % (l + 1), "list%d.1" % (l + 1)]
            if l == 0:
                emit("v", lambda: v.tensor_copy(T.wt[:], win), ll, ["wt"])
            else:
                tt(T.wt[:], win, D0[:], OP.add, [mp["d0"]] + ll, ["wt"])

        level(0, 1, 2)
        if r > 0:
            unpack(2)
            unpack(3)
        else:
            const_m(2)
            const_p(2)
            const_m(3)
        list_mm(3, 1, 3)
        lev_mm(2, 1, 2)
        if r == 0:
            for b in range(4):
                quant("e%d" % b, 0, 128, T.idt[:, 4 - b:516 - b], ["idt"], ["qe%d" % b])
            for j in range(4):
                unpack(j)
        for h in range(2):
            for gg in range(8):
                e = 16 * SOURCE[gg]
                dma("sy", T.fp[16 * gg:16 * gg + 16, 4 * C * h:4 * C * h + 4 * C], T.fh[e:e + 16, :], fhk, ["fp.%d" % (8 * h + gg)], "fpd", True)
        level(1, 4, 5)
        lev_mm(3, 4, None)
        level(2, 1, 2)
        if r == 0:
            ts(T.mask16[:], T.j16[:], col("q"), -1.0, OP.is_equal, OP.mult, ["j16", "c.q"], ["mask16"])
        level(3, 4, None)
        for h in range(2):
            c = slice(144 * h, 144 * h + 144)
            tt(T.ex[:, c], T.t[:, c], T.mask16[:, c], OP.mult, Tk + ["mask16"], ["ex.%d" % h])
            scan(T.scx[:, c], T.r16[:, c], T.ex[:, c], 0.0, OP.mult, OP.add, ["r16", "ex.%d" % h], ["scx.%d" % h])
        for a in range(NA):
            emit("a", lambda a=a: s_.activation(T.junk[:, C * a:C * a + C], T.t[:], AF.Sign, bias=T.scx[:, 16 * a + 15:16 * a + 16],
                                                accum_out=T.acc[:, a:a + 1]), Tk + ["scx.%d" % (a // 9)], ["acc.%d" % a])

        def cmp_scan(j):
            scan(T.cs[:, C * j:C * j + C], T.r144[:], T.cf[:, C * j:C * j + C], 0.0, OP.mult, OP.add, ["r144", "cf.%d" % j], ["cs.%d" % j])
        for j in range(NV):
            a = NA + j
            ts(T.cf[:, C * j:C * j + C], T.t[:], T.scx[:, 16 * a + 15:16 * a + 16], 0.0, OP.add, OP.is_lt, Tk + ["scx.1"], ["cf.%d" % j])
            if j > 0:
                cmp_scan(j - 1)
        x1, y1, lo, z, e1, e2 = [T.sm[:, i:i + 1] for i in range(6)]
        tt(lo, x1, y1, OP.subtract, ["x1", "y1"], ["lo"])
        cmp_scan(NV - 1)
        ts(z, lo, magic(64), magic(64), OP.add, OP.subtract, ["lo"], ["z"])
        ts(e1, lo, 512.0 * mp["al"], 512.0 * (mp["ga"] + 288.0), OP.mult, OP.add, ["lo"], ["e1"])
        tt(T.rkv[:], T.cs[:, 143:NV * C:288], T.cs[:, 287:NV * C:288], OP.add, ["cs.%d" % j for j in range(NV)], ["rkv"])
        ts(e2, z, -512.0 * mp["be"], e1, OP.mult, OP.add, ["z", "e1"], ["e2"])
        emit("v", lambda: v.tensor_copy(T.off[:, NA:18], T.rkv[:]), ["rkv"], ["off.v"])
        ts(T.bcb[:], T.thr3[:], x1, e2, OP.is_gt, OP.mult, ["thr3", "x1", "e2"], ["bcb"])
        emit("v", lambda: v.transpose(T.trb[:], T.bcb[:]), ["bcb"], ["trb"])
        tt(T.val[:], T.trb[:, 0:32].indirect(T.list3[:, 0:18]), T.own[:], OP.add, ["trb", "own", "list3.0", "list3.1"], ["val"])
        if r == 0:
            cs("eo", "e", 576.0, None, OP.add, None)
            ts(T.mask4[:], T.j4[:], col("k4"), None, OP.is_equal, None, ["j4", "c.k4"], ["mask4"])
        ts(T.off[:, 0:NA], T.acc[:], -0.5, 143.5, OP.mult, OP.add, ["acc.%d" % a for a in range(NA)], ["off.a"])
        emit("v", lambda: v.tensor_copy(T.lin[:, 0:C].indirect(T.off[:, 0:18]), T.val[:]), ["off.a", "off.v", "val"], ["lin"])
        tt(T.ml[:, 0:K], T.lin[:, 0:K], T.mask4[:, 0:K], OP.mult, ["lin", "mask4"], ["ml.0"])
        scan(T.sc[:, 0:K], T.r4[:, 0:K], T.ml[:, 0:K], 0.0, OP.mult, OP.add, ["r4", "ml.0"], ["sc.0"])
        W = T.sc[:, 3:K:4]
        ts(T.ta[:, 0:32], W, magic(512), magic(512), OP.add, OP.subtract, ["sc.0"], ["ta"])
        tt(T.oa[:, 0:32], W, T.ta[:, 0:32], OP.subtract, ["sc.0", "ta"], ["oa"])
        ts(T.lu[:], T.oa[:, 0:32], 4.0, col("eo"), OP.mult, OP.add, ["oa", "c.eo"], ["lu"])
        for h in range(2):
            act(T.g1[:, 256 * h:256 * h + 256], T.fh[:, 0:4 * C].indirect(T.lu[:, 16 * h:16 * h + 16]), fhk + ["lu"], ["g1.%d" % h])
        ts(T.la[:], T.oa[:, 0:32], 4.0, col("eo"), OP.mult, OP.add, ["oa", "c.eo"], ["la"])
        ts(T.lb[:], T.ta[:, 0:32], 1.0 / 128.0, col("e"), OP.mult, OP.add, ["ta", "c.e"], ["lb"])
        tt(T.lb[:], T.lb[:], T.la[:], OP.max, ["lb", "la"], ["lb"])
        emit("v", lambda: v.tensor_copy(T.bu[:], T.lb[:]), ["lb"], ["bu"])
        for h in range(2):
            tt(T.zt[:, 256 * h:256 * h + 256], T.fp[:, 0:8 * C].indirect(T.bu[:, 16 * h:16 * h + 16]), T.g1[:, 256 * h:256 * h + 256], OP.add,
               fpk + ["bu", "g1.%d" % h], ["zt.%d" % h])
        quant("z", K * r, K * r + K, T.zt[:], ["zt.0", "zt.1"], ["qz%d" % r])

        def send():
            z = slice(K * r, K * r + K)
            if direct:
                es, sem = topo.engines(core, nxt)[:8], T.sem["arr%d" % r]
                g.remote_dma_fused([move(topo, core, nxt, es, sem, u8(T.qa[:, z]), u8(T.qz[:, z]))], local_sem=T.sem.snt)
                g.remote_dma_fused([move(topo, core, nxt, es, sem, T.sa[:, z], T.sz[:, z])], local_sem=T.sem.snt)
                sent.append(2 * len(es))
                return
            sem = T.sem["rar%d" % r]
            es = topo.engines(core, hopmates[0])
            m = len(es) // 2
            g.remote_dma_fused([move(topo, core, hopmates[j], es[m * j:m * j + m], sem, u8(T.rq[:, 64 * r:64 * r + 64]),
                                     u8(T.qz[:, K * r + 64 * j:K * r + 64 * j + 64])) for j in range(2)], local_sem=T.sem.snt)
            g.remote_dma_fused([move(topo, core, hopmates[2], es, sem, T.rs[:, z], T.sz[:, z])], local_sem=T.sem.snt)
            sent.append(2 * len(es))
        emit("g", send, ["qz%d" % r], [])

        tt(T.ml[:, K:C], T.lin[:, K:C], T.mask4[:, K:C], OP.mult, ["lin", "mask4"], ["ml.1"])
        scan(T.sc[:, K:C], T.r4[:, K:C], T.ml[:, K:C], 0.0, OP.mult, OP.add, ["r4", "ml.1"], ["sc.1"])
        W2 = T.sc[:, K + 3:C:4]
        ts(T.tsv[:], W2, magic(512), magic(512), OP.add, OP.subtract, ["sc.1"], ["tsv"])
        tt(T.osv[:], W2, T.tsv[:], OP.subtract, ["sc.1", "tsv"], ["osv"])
        ts(T.sul[:], T.osv[:], 4.0, col("eo"), OP.mult, OP.add, ["osv", "c.eo"], ["sul"])
        act(T.xs[:, 0:320], T.fh[:, 0:4 * C].indirect(T.sul[:, 0:20]), fhk + ["sul"], ["xs"], scale=2.0)
        ts(T.xs[:, 320:640], T.fh[:, 0:4 * C].indirect(T.sul[:, 20:40]), 2.0, None, OP.mult, None, fhk + ["sul"], ["xs.v"])
        quant("x", 0, NS, T.xs[:], ["xs", "xs.v"], ["qxs"])
        if r < R - 1:
            front(0)
            for l in (1, 2, 3):
                list_mm(l, 0, l)
            for l in (1, 2, 3):
                list_out(l, 0, l)
            mm(4, NS, "m0", 0, "f", 10, ["qm0", "qfs"])
            mm(5, NS, "p0", 0, "f", 10, ["qp0", "qfs"])
            for k in range(8):
                scan(T.t[:, k:NS:8], T.zf[:, k:NS:8], T.ps4[:, k:NS:8], -1.0e6, OP.max, OP.add, ["zf", "ps4"], [Tk[k], "th.%d" % k])
            tt(T.pv[:, 0:NS], T.t[:, 0:NS], T.ps5[:, 0:NS], OP.add, Tk + ["ps5"], ["pvs"])
            emit("v", lambda: v.tensor_reduce(T.sm[:, 8:9], T.pv[:, 0:NS], AxisListType.X, OP.min), ["pvs"], ["xs1"])
        else:
            ts(T.jn[:], T.jn[:], col("q"), None, OP.add, None, ["jn", "c.q"], ["jn"])
            ts(T.jk[:], T.jn[:], 1.0 / 36.0, -17.5 / 36.0, OP.mult, OP.add, ["jn"], ["jk"])
            ts(T.jk[:], T.jk[:], magic(1), magic(1), OP.add, OP.subtract, ["jk"], ["jk"])
            ts(T.jk[:], T.jk[:], -287.0, None, OP.mult, None, ["jk"], ["jk"])
            ts(T.jn[:], T.jn[:], 8.0, None, OP.mult, None, ["jn"], ["jn"])
            tt(T.jn[:], T.jn[:], T.jk[:], OP.add, ["jn", "jk"], ["jn"])
            emit("v", lambda: v.tensor_copy(T.nat[:], T.jn[:]), ["jn"], ["nat"])
            quant("v", 0, 128, T.vt[:], ["vt"], ["qv"])
            ts(T.o1[:], T.lin[:], magic(512), magic(512), OP.add, OP.subtract, ["lin"], ["o1"])
            tt(T.o2[:], T.lin[:], T.o1[:], OP.subtract, ["lin", "o1"], ["o2"])
            ts(T.o3[:], T.o2[:], 140.5, magic(8), OP.add, OP.add, ["o2"], ["o3"])
            ts(T.o1[:], T.o2[:], 36.0, 5184.0, OP.mult, OP.add, ["o2"], ["o1"])
            ts(T.o4[:], T.o3[:], magic(8), -35.875, OP.subtract, OP.mult, ["o3"], ["o4"])
            tt(T.opt[:], T.o1[:], T.o4[:], OP.add, ["o1", "o4"], ["opt"])
            dma("sy", T.op[:], T.opt[0:128:16, :], ["opt"], [], "od")

        ne = 3 * len(topo.engines(indirect_in[0], core)) if indirect_in else 16
        g.tensor.wait_ge(T.sem["arr%d" % r], ne)
        for b in range(4):
            mm(b, K, "w", 128 * b, "a", K * r, ["qw", "sw"], stop=False)
            mm(b, K, "e%d" % b, 0, "a", K * r, ["qe%d" % b], start=False)
            if b % 2 == 0:
                act(T.xh[:, b:512:4], T["ps%d" % b][:, 0:K], ["ps%d" % b], ["xh.%d" % b], scale=0.0078125)
            else:
                ts(T.xh[:, b:512:4], T["ps%d" % b][:, 0:K], 0.0078125, None, OP.mult, None, ["ps%d" % b], ["xh.%d" % b])
        quant("x", NS, C, T.xh[:], ["xh.%d" % b for b in range(4)], ["qxh"])

    emit("v", lambda: v.tensor_copy(T.qn[:, 0:C].bitcast(dt.uint32), T.qx[:, 0:C].bitcast(dt.uint32).indirect(T.nat[:, 0:18])), qx + ["nat"], ["qn"])
    emit("a", lambda: s_.activation(T.sn[:, 0:C], T.sx[:, 0:C].indirect(T.nat[:, 0:18]), CP), qx + ["nat"], ["sn"])
    mm(0, C, "v", 0, "n", 0, ["qv", "qn", "sn"])
    dma("sy", T.oc[:], u8(T.qn[:]), ["qn"], [], "od")
    for k in range(4):
        dma("a", T.osc[4 * k:4 * k + 4, :], T.sn[32 * k:32 * k + 4, :], ["sn"], [], "od")
    emit("v", lambda: v.tensor_copy(T.yt[:], T.ps0[:, 0:C]), ["ps0"], ["yt"])
    dma("sy", T.y[:], T.yt[:], ["yt"], [], "od")
    for s in count:
        g.wait_ge(T.sem[s], count[s])
    g.wait_ge(T.sem.snt, sum(sent))
